import numpy as np
import ml_dtypes


def mxq(x, axis, fmt="e4m3"):
    dtype, down = {"e4m3": (ml_dtypes.float8_e4m3fn, 7), "e5m2": (ml_dtypes.float8_e5m2, 14)}[fmt]
    v = np.moveaxis(np.asarray(x, np.float32).astype(ml_dtypes.bfloat16).astype(np.float64), axis, -1)
    blocks = v.reshape(v.shape[:-1] + (-1, 32))
    amax = np.abs(blocks).max(-1, keepdims=True)
    byte = np.maximum(np.where(amax > 0, np.frexp(amax)[1] - 1 + 127, 0) - down, 1)
    scale = np.exp2(byte - 127.0)
    codes = (blocks / scale).astype(np.float32).astype(dtype).astype(np.float64)
    return np.moveaxis((codes * scale).reshape(v.shape), -1, axis)


WIDE = False


def mx_kscale(k):
    if not WIDE:
        return np.ones(k)
    levels = np.array([10, -10, 5, -5, 0])
    if k % 512:
        return np.exp2(np.random.permutation(np.resize(levels, k // 32))).repeat(32)
    a = np.empty((k // 512, 16))
    for p in range(k // 512):
        a[p, :8] = np.random.permutation(np.resize(levels, 8))
        for g in range(8):
            far = levels[np.abs(levels - a[p, g]) >= 10]
            a[p, g + 8] = far[np.random.randint(len(far))]
    return np.exp2(a.ravel()).repeat(32)


def f64(x):
    return np.asarray(x).astype(np.float64)


def striped(idx):
    return np.tile(idx.reshape(-1, 16).T, (8, 1)).astype(np.uint16)


def unstriped(offs):
    return offs[:16].T.reshape(-1).astype(np.int64)


E2M1 = np.array([0.0, 0.5, 1.0, 1.5, 2.0, 3.0, 4.0, 6.0, -0.0, -0.5, -1.0, -1.5, -2.0, -3.0, -4.0, -6.0])


def pack_weight(w, fmt):
    k, n = w.shape
    w = f64(np.asarray(w, np.float32).astype(ml_dtypes.bfloat16)).reshape(k // 32, 32, n)
    amax = np.abs(w).max(1)
    if fmt == "e4m3":
        byte = np.frexp(amax)[1] - 1 + 127 - 7
    else:
        mant, ex = np.frexp(amax / 6.0)
        byte = np.where(mant > 0.5, ex, ex - 1) + 127
    byte = np.clip(np.where(amax > 0, byte, 1), 1, 254)
    scaled = (w * np.exp2(127.0 - byte)[:, None, :]).reshape(k, n).astype(np.float32)
    by_word = np.ascontiguousarray(scaled.reshape(k // 512, 128, 4, n).transpose(0, 1, 3, 2))
    if fmt == "e4m3":
        words = by_word.astype(ml_dtypes.float8_e4m3fn).view(np.uint8)
    else:
        c = by_word.astype(ml_dtypes.float4_e2m1fn).view(np.uint8) & 0xF
        words = (c[..., 0::2] | (c[..., 1::2] << 4)).reshape(k // 512, 128, 2 * n)
    return np.ascontiguousarray(words), np.ascontiguousarray(byte.astype(np.uint8).reshape(k // 512, 16, n))


def unpack_weight(words, scales, fmt):
    g, _, n = scales.shape
    words = np.ascontiguousarray(words).reshape(g, 128, n, -1)
    if fmt == "e4m3":
        vals = words.view(ml_dtypes.float8_e4m3fn).astype(np.float64)
    else:
        nib = np.empty((g, 128, n, 4), np.uint8)
        nib[..., 0::2] = words & 0xF
        nib[..., 1::2] = words >> 4
        vals = E2M1[nib]
    vals = vals * np.repeat(np.exp2(scales.astype(np.float64) - 127.0), 8, axis=1)[..., None]
    return vals.transpose(0, 1, 3, 2).reshape(g * 512, n)


def gelu(v):
    return 0.5 * v * (1.0 + np.tanh(np.sqrt(2.0 / np.pi) * (v + 0.044715 * v**3)))


K, T, E, C, H, N = 1024, 1024, 4, 256, 512, 512


def by_expert(wq, xq):
    return np.concatenate([wq[e].T @ xq[:, e * C:(e + 1) * C] for e in range(E)], axis=1)


def setup_inputs():
    n = np.random.standard_normal
    s = mx_kscale(K)
    u = mx_kscale(H)
    slot_token = np.random.permutation(T)[:E * C]
    x = pack_weight(n((K, T)) * s[:, None], "e4m3")
    w1 = [pack_weight(m, "e2m1") for m in n((E, K, H)) / np.sqrt(K) / s[None, :, None] * u]
    w2 = pack_weight(n((H, N)) / np.sqrt(H) / u[:, None], "e2m1")
    return {
        "x_words": x[0],
        "x_scales": x[1],
        "w1_words": np.stack([m[0] for m in w1]),
        "w1_scales": np.stack([m[1] for m in w1]),
        "w2_words": w2[0],
        "w2_scales": w2[1],
        "gate": np.tile(np.random.uniform(0.2, 1.0, E * C), (128, 1)).astype(np.float32),
        "offs": striped(slot_token),
    }


def reference(x_words, x_scales, w1_words, w1_scales, w2_words, w2_scales, gate, offs):
    w1 = np.stack([unpack_weight(w1_words[e], w1_scales[e], "e2m1") for e in range(E)])
    w2 = unpack_weight(w2_words, w2_scales, "e2m1")
    idx = unstriped(offs)
    xq = unpack_weight(x_words, x_scales, "e4m3")[:, idx]
    h = gelu(by_expert(w1, xq))
    c = np.zeros((H, T))
    c[:, idx] = f64(gate[:1]) * h
    return w2.T @ mxq(c, 0, "e4m3")

@@ -1,0 +1,190 @@
+from contextlib import ExitStack
+
+import concourse.mybir as mybir
+from concourse.masks import make_identity
+
+K, T, E, C, H, N = 1024, 1024, 4, 256, 512, 512
+FLOPS = 2 * K * H * E * C + 2 * H * N * T
+
+F32 = mybir.dt.float32
+BF16 = mybir.dt.bfloat16
+I32 = mybir.dt.int32
+U32 = mybir.dt.uint32
+U16 = mybir.dt.uint16
+U8 = mybir.dt.uint8
+FP8X4 = mybir.dt.float8_e4m3fn_x4
+FP4X4 = mybir.dt.float4_e2m1fn_x4
+ACT = mybir.ActivationFunctionType
+ALU = mybir.AluOpType
+
+P = 128
+PACK = 4
+PASSES = K // (P * PACK)
+LIST_ROWS = 16
+SCALE_ROWS = 4
+QUADRANT = 32
+SHIFTED = 112
+CHUNK = 256
+HALF = T // 2
+
+
+def load_scale_rows(nc, plane, rows):
+    for r in range(SCALE_ROWS):
+        nc.sync.dma_start(out=plane[:].bitcast(I32)[r:P:QUADRANT], in_=rows.bitcast(I32)[r:16:SCALE_ROWS])
+
+
+def tile_moe_sdn_lin_gelu_kernel(
+    tc, x_words, x_scales, w1_words, w1_scales, w2_words, w2_scales, gate, offs, out
+):
+    nc = tc.nc
+    with ExitStack() as ctx:
+        keep = ctx.enter_context(tc.tile_pool(name="keep", bufs=1))
+        ring = ctx.enter_context(tc.tile_pool(name="ring", bufs=3))
+        ps_h = ctx.enter_context(tc.psum_pool(name="ps_h", bufs=2))
+        ps_t = ctx.enter_context(tc.psum_pool(name="ps_t", bufs=2))
+        ps_o = ctx.enter_context(tc.psum_pool(name="ps_o", bufs=4))
+
+        offsets = keep.tile([P, T // LIST_ROWS], U16, name="offsets")
+        x_plane = keep.tile([P, T], U8, name="x_plane", align_bytes=64)
+        w1_plane = keep.tile([P, E * PASSES, H], U8, name="w1_plane", align_bytes=64)
+        w2_plane = keep.tile([P, 1, N], U8, name="w2_plane", align_bytes=64)
+        x_sb = [keep.tile([P, T], I32, name="x_sb%d" % s, align_bytes=64) for s in range(PASSES)]
+        w1_sb = [keep.tile([P, PASSES, 2 * H], U8, name="w1_sb%d" % e, align_bytes=64) for e in range(E)]
+        w2_sb = keep.tile([P, 2 * N], U8, name="w2_sb", align_bytes=64)
+        gate_sb = keep.tile([P, T], F32, name="gate_sb")
+        identity = keep.tile([P, P], F32, name="identity")
+        staged = keep.tile([P, PACK, T], F32, name="staged")
+        planes = [keep.tile([P, T], F32, name="plane%d" % d, align_bytes=64) for d in range(PACK)]
+        got_scales = [keep.tile([P, HALF], U8, name="got_scales%d" % a, align_bytes=64) for a in range(2)]
+        moved_scales = [keep.tile([P, HALF], U8, name="moved_scales%d" % a, align_bytes=64) for a in range(2)]
+
+        nc.vector.memset(x_plane[:].bitcast(I32), 0)
+        nc.vector.memset(w1_plane[:].bitcast(I32), 0)
+        for a in range(2):
+            nc.vector.memset(moved_scales[a][:].bitcast(I32), 0)
+        nc.vector.memset(w2_plane[:].bitcast(I32), 0)
+        make_identity(nc, identity[:])
+
+        nc.sync.dma_start(offsets[:], offs)
+        x_rows = x_scales.bitcast(I32)
+        for q in range(P // QUADRANT):
+            nc.sync.dma_start(
+                out=x_plane[:].bitcast(I32)[QUADRANT * q : QUADRANT * q + PASSES * SCALE_ROWS],
+                in_=x_rows[:, SCALE_ROWS * q : SCALE_ROWS * (q + 1), :],
+            )
+        for s in range(PASSES):
+            nc.sync.dma_start(out=x_sb[s][:], in_=x_words[s].rearrange("p t d -> p (t d)").bitcast(I32))
+
+        def load_w1(e):
+            nc.sync.dma_start(
+                out=w1_sb[e][:].bitcast(I32), in_=w1_words[e].rearrange("s p b -> p s b").bitcast(I32)
+            )
+
+        load_w1(0)
+        load_scale_rows(nc, w1_plane, w1_scales.rearrange("e s b i -> b (e s) i"))
+        load_w1(1)
+        nc.sync.dma_start(out=gate_sb[:], in_=gate)
+        for e in range(2, E):
+            load_w1(e)
+        nc.sync.dma_start(out=w2_sb[:].bitcast(I32), in_=w2_words[0].bitcast(I32))
+        load_scale_rows(nc, w2_plane, w2_scales.rearrange("s b n -> b s n"))
+
+        def listed(lo, hi):
+            return offsets[:, lo // LIST_ROWS : hi // LIST_ROWS]
+
+        for a in range(2):
+            nc.vector.tensor_copy(got_scales[a][:], x_plane[:].indirect(listed(a * HALF, (a + 1) * HALF)))
+            nc.scalar.dma_start(
+                out=moved_scales[a][:].bitcast(I32)[0:SHIFTED],
+                in_=got_scales[a][:].bitcast(I32)[SCALE_ROWS : SCALE_ROWS + SHIFTED],
+            )
+
+        got_words = {}
+        for lo, hi in ((0, C), (C, 2 * C), (2 * C, T)):
+            for s in range(PASSES):
+                words = keep.tile([P, hi - lo], U32, name="got_words%d_%d" % (lo, s), align_bytes=64)
+                nc.vector.tensor_copy(words[:], x_sb[s][:].bitcast(U32).indirect(listed(lo, hi)))
+                for j0 in range(lo, hi, P):
+                    got_words[j0, s] = words[:, j0 - lo : j0 - lo + P]
+
+        gate_cols = keep.tile([P, T // P], F32, name="gate_cols")
+        for b in range(2):
+            gate_ps = ps_t.tile([P, PACK, P], F32, name="turned")
+            for j in range(PACK):
+                nc.tensor.transpose(gate_ps[:, j, :], gate_sb[:, (4 * b + j) * P : (4 * b + j + 1) * P], identity[:])
+            nc.scalar.copy(gate_cols[:, 4 * b : 4 * b + 4], gate_ps[:, :, 0])
+
+        for j0 in range(0, T, P):
+            e = j0 // C
+            cols = slice(j0 % HALF, j0 % HALF + P)
+            acc = ps_h.tile([P, H], F32, name="acc")
+            for s, scales in enumerate((got_scales, moved_scales)):
+                nc.tensor.matmul_mx(
+                    out=acc[:],
+                    lhsT=got_words[j0, s].bitcast(FP8X4),
+                    lhsT_scale=scales[j0 // HALF][:, cols],
+                    rhs=w1_sb[e][:, s, :].bitcast(FP4X4),
+                    rhs_scale=w1_plane[:, e * PASSES + s, :],
+                    start=(s == 0),
+                    stop=(s == PASSES - 1),
+                )
+            h = ring.tile([P, PACK, P], F32, name="h")
+            nc.scalar.activation(h[:], acc[:].rearrange("p (q d) -> p d q", d=PACK), ACT.Gelu_apprx_tanh)
+            hg = ring.tile([P, 2, P], F32, name="hg")
+            nc.scalar.activation(hg[:], h[:, 2:4, :], ACT.Copy, scale=gate_cols[:, j0 // P : j0 // P + 1])
+            turned = ps_t.tile([P, PACK, P], F32, name="turned")
+            for d in range(PACK):
+                nc.tensor.transpose(turned[:, d, :], (h[:, d, :] if d < 2 else hg[:, d - 2, :]), identity[:])
+            nc.scalar.copy(staged[:, :, j0 : j0 + P], turned[:])
+
+        def scatter(d, lo, hi):
+            if d >= 2:
+                nc.vector.tensor_copy(planes[d][:].indirect(listed(lo, hi)), staged[:, d, lo:hi])
+                return
+            nc.vector.tensor_tensor(
+                planes[d][:].indirect(listed(lo, hi)), staged[:, d, lo:hi], gate_sb[:, lo:hi], ALU.mult
+            )
+
+        chunks = [slice(t0, t0 + CHUNK) for t0 in range(0, T, CHUNK)]
+        c_tok = keep.tile([P, T, PACK], BF16, name="c_tok", align_bytes=64)
+
+        for d in range(PACK):
+            scatter(d, 0, P)
+        for d in range(2):
+            scatter(d, P, HALF)
+        for d in range(2):
+            scatter(d, HALF, T)
+            nc.scalar.copy(c_tok[:, :, d], planes[d][:])
+        scatter(2, P, HALF)
+        scatter(2, HALF, T)
+        nc.scalar.copy(c_tok[:, :, 2:4], planes[2][:].unsqueeze(2).to_broadcast([P, T, 2]))
+        scatter(3, P, HALF)
+        scatter(3, HALF, T)
+
+        out_view = out.rearrange("(m p) t -> p m t", p=P)
+        for toks in chunks:
+            nc.vector.tensor_copy(c_tok[:, toks, 3], planes[3][:, toks])
+            c_words = keep.tile([P, CHUNK], U32, name="c_words%d" % toks.start, align_bytes=64)
+            c_scales = keep.tile([P, CHUNK], U8, name="c_scales%d" % toks.start, align_bytes=64)
+            nc.vector.quantize_mx(
+                out=c_words[:].bitcast(FP8X4), scales=c_scales[:], in_=c_tok[:, toks, :].rearrange("p t d -> p (t d)")
+            )
+            for m0 in range(0, N // P, 2):
+                acc2 = ps_o.tile([P, 2, CHUNK], F32, name="acc2")
+                for j in range(2):
+                    m = m0 + j
+                    nc.tensor.matmul_mx(
+                        out=acc2[:, j, :],
+                        lhsT=w2_sb[:, 2 * P * m : 2 * P * (m + 1)].bitcast(FP4X4),
+                        lhsT_scale=w2_plane[:, 0, P * m : P * (m + 1)],
+                        rhs=c_words[:].bitcast(FP8X4),
+                        rhs_scale=c_scales[:],
+                        start=True,
+                        stop=True,
+                    )
+                res = keep.tile([P, 2, CHUNK], F32, name="res%d_%d" % (toks.start, m0))
+                if toks.stop == T and m0 > 0:
+                    nc.vector.tensor_copy(res[:], acc2[:])
+                else:
+                    nc.scalar.copy(res[:], acc2[:])
+                nc.sync.dma_start(out=out_view[:, m0 : m0 + 2, toks], in_=res[:])

@@ -24,8 +24,12 @@ LIST_ROWS = 16
 SCALE_ROWS = 4
 QUADRANT = 32
 SHIFTED = 112
-CHUNK = 256
+BANK = 512
 HALF = T // 2
+BYTE_CUTS = ((0, C), (C, T))
+WORD_CUTS = ((0, C), (C, HALF), (HALF, T))
+CHUNKS = ((0, 256, (1, 1, 2)), (256, 256, (2, 2)), (512, 256, (2, 2)), (768, 256, (2, 2)))
+ON_VECTOR = (6, 8)
 
 
 def load_scale_rows(nc, plane, rows):
@@ -48,20 +52,36 @@ def tile_moe_sdn_lin_gelu_kernel(
         x_plane = keep.tile([P, T], U8, name="x_plane", align_bytes=64)
         w1_plane = keep.tile([P, E * PASSES, H], U8, name="w1_plane", align_bytes=64)
         w2_plane = keep.tile([P, 1, N], U8, name="w2_plane", align_bytes=64)
-        x_sb = [keep.tile([P, T], I32, name="x_sb%d" % s, align_bytes=64) for s in range(PASSES)]
-        w1_sb = [keep.tile([P, PASSES, 2 * H], U8, name="w1_sb%d" % e, align_bytes=64) for e in range(E)]
+        x_sb = keep.tile([P, PASSES, T], I32, name="x_sb", align_bytes=64)
+        w1_sb = keep.tile([P, E, PASSES, 2 * H], U8, name="w1_sb", align_bytes=64)
         w2_sb = keep.tile([P, 2 * N], U8, name="w2_sb", align_bytes=64)
         gate_sb = keep.tile([P, T], F32, name="gate_sb")
         identity = keep.tile([P, P], F32, name="identity")
         staged = keep.tile([P, PACK, T], F32, name="staged")
         planes = [keep.tile([P, T], F32, name="plane%d" % d, align_bytes=64) for d in range(PACK)]
-        got_scales = [keep.tile([P, HALF], U8, name="got_scales%d" % a, align_bytes=64) for a in range(2)]
-        moved_scales = [keep.tile([P, HALF], U8, name="moved_scales%d" % a, align_bytes=64) for a in range(2)]
+        got_scales = [keep.tile([P, hi - lo], U8, name="got_scales%d" % lo, align_bytes=64) for lo, hi in BYTE_CUTS]
+        moved_scales = [keep.tile([P, hi - lo], U8, name="moved_scales%d" % lo, align_bytes=64) for lo, hi in BYTE_CUTS]
+
+        def load_w1(e):
+            nc.sync.dma_start(
+                out=w1_sb[:, e].bitcast(I32), in_=w1_words[e].rearrange("s p b -> p s b").bitcast(I32)
+            )
+
+        def listed(lo, hi):
+            return offsets[:, lo // LIST_ROWS : hi // LIST_ROWS]
+
+        def gather_scales(a):
+            lo, hi = BYTE_CUTS[a]
+            nc.vector.tensor_copy(got_scales[a][:], x_plane[:].indirect(listed(lo, hi)))
+            nc.sync.dma_start(
+                out=moved_scales[a][:].bitcast(I32)[0:SHIFTED],
+                in_=got_scales[a][:].bitcast(I32)[SCALE_ROWS : SCALE_ROWS + SHIFTED],
+            )
 
         nc.vector.memset(x_plane[:].bitcast(I32), 0)
         nc.vector.memset(w1_plane[:].bitcast(I32), 0)
-        for a in range(2):
-            nc.vector.memset(moved_scales[a][:].bitcast(I32), 0)
+        for moved in moved_scales:
+            nc.vector.memset(moved[:].bitcast(I32), 0)
         nc.vector.memset(w2_plane[:].bitcast(I32), 0)
         make_identity(nc, identity[:])
 
@@ -72,80 +92,53 @@ def tile_moe_sdn_lin_gelu_kernel(
                 out=x_plane[:].bitcast(I32)[QUADRANT * q : QUADRANT * q + PASSES * SCALE_ROWS],
                 in_=x_rows[:, SCALE_ROWS * q : SCALE_ROWS * (q + 1), :],
             )
-        for s in range(PASSES):
-            nc.sync.dma_start(out=x_sb[s][:], in_=x_words[s].rearrange("p t d -> p (t d)").bitcast(I32))
-
-        def load_w1(e):
-            nc.sync.dma_start(
-                out=w1_sb[e][:].bitcast(I32), in_=w1_words[e].rearrange("s p b -> p s b").bitcast(I32)
-            )
-
+        nc.sync.dma_start(out=x_sb[:], in_=x_words.rearrange("s p t d -> p s (t d)").bitcast(I32))
         load_w1(0)
         load_scale_rows(nc, w1_plane, w1_scales.rearrange("e s b i -> b (e s) i"))
+        gather_scales(0)
         load_w1(1)
+        gather_scales(1)
         nc.sync.dma_start(out=gate_sb[:], in_=gate)
         for e in range(2, E):
             load_w1(e)
         nc.sync.dma_start(out=w2_sb[:].bitcast(I32), in_=w2_words[0].bitcast(I32))
         load_scale_rows(nc, w2_plane, w2_scales.rearrange("s b n -> b s n"))
 
-        def listed(lo, hi):
-            return offsets[:, lo // LIST_ROWS : hi // LIST_ROWS]
-
-        for a in range(2):
-            nc.vector.tensor_copy(got_scales[a][:], x_plane[:].indirect(listed(a * HALF, (a + 1) * HALF)))
-            nc.scalar.dma_start(
-                out=moved_scales[a][:].bitcast(I32)[0:SHIFTED],
-                in_=got_scales[a][:].bitcast(I32)[SCALE_ROWS : SCALE_ROWS + SHIFTED],
-            )
-
         got_words = {}
-        for lo, hi in ((0, C), (C, 2 * C), (2 * C, T)):
+        for lo, hi in WORD_CUTS:
             for s in range(PASSES):
                 words = keep.tile([P, hi - lo], U32, name="got_words%d_%d" % (lo, s), align_bytes=64)
-                nc.vector.tensor_copy(words[:], x_sb[s][:].bitcast(U32).indirect(listed(lo, hi)))
+                nc.vector.tensor_copy(words[:], x_sb[:, s, :].bitcast(U32).indirect(listed(lo, hi)))
                 for j0 in range(lo, hi, P):
                     got_words[j0, s] = words[:, j0 - lo : j0 - lo + P]
 
-        gate_cols = keep.tile([P, T // P], F32, name="gate_cols")
-        for b in range(2):
-            gate_ps = ps_t.tile([P, PACK, P], F32, name="turned")
-            for j in range(PACK):
-                nc.tensor.transpose(gate_ps[:, j, :], gate_sb[:, (4 * b + j) * P : (4 * b + j + 1) * P], identity[:])
-            nc.scalar.copy(gate_cols[:, 4 * b : 4 * b + 4], gate_ps[:, :, 0])
-
         for j0 in range(0, T, P):
             e = j0 // C
-            cols = slice(j0 % HALF, j0 % HALF + P)
+            a = min(e, 1)
+            cols = slice(j0 - BYTE_CUTS[a][0], j0 - BYTE_CUTS[a][0] + P)
             acc = ps_h.tile([P, H], F32, name="acc")
             for s, scales in enumerate((got_scales, moved_scales)):
                 nc.tensor.matmul_mx(
                     out=acc[:],
                     lhsT=got_words[j0, s].bitcast(FP8X4),
-                    lhsT_scale=scales[j0 // HALF][:, cols],
-                    rhs=w1_sb[e][:, s, :].bitcast(FP4X4),
+                    lhsT_scale=scales[a][:, cols],
+                    rhs=w1_sb[:, e, s, :].bitcast(FP4X4),
                     rhs_scale=w1_plane[:, e * PASSES + s, :],
                     start=(s == 0),
                     stop=(s == PASSES - 1),
                 )
             h = ring.tile([P, PACK, P], F32, name="h")
             nc.scalar.activation(h[:], acc[:].rearrange("p (q d) -> p d q", d=PACK), ACT.Gelu_apprx_tanh)
-            hg = ring.tile([P, 2, P], F32, name="hg")
-            nc.scalar.activation(hg[:], h[:, 2:4, :], ACT.Copy, scale=gate_cols[:, j0 // P : j0 // P + 1])
             turned = ps_t.tile([P, PACK, P], F32, name="turned")
             for d in range(PACK):
-                nc.tensor.transpose(turned[:, d, :], (h[:, d, :] if d < 2 else hg[:, d - 2, :]), identity[:])
+                nc.tensor.transpose(turned[:, d, :], h[:, d, :], identity[:])
             nc.scalar.copy(staged[:, :, j0 : j0 + P], turned[:])
 
         def scatter(d, lo, hi):
-            if d >= 2:
-                nc.vector.tensor_copy(planes[d][:].indirect(listed(lo, hi)), staged[:, d, lo:hi])
-                return
             nc.vector.tensor_tensor(
                 planes[d][:].indirect(listed(lo, hi)), staged[:, d, lo:hi], gate_sb[:, lo:hi], ALU.mult
             )
 
-        chunks = [slice(t0, t0 + CHUNK) for t0 in range(0, T, CHUNK)]
         c_tok = keep.tile([P, T, PACK], BF16, name="c_tok", align_bytes=64)
 
         for d in range(PACK):
@@ -161,17 +154,21 @@ def tile_moe_sdn_lin_gelu_kernel(
         scatter(3, P, HALF)
         scatter(3, HALF, T)
 
+
         out_view = out.rearrange("(m p) t -> p m t", p=P)
-        for toks in chunks:
+        store_no = 0
+        for t0, width, groups in CHUNKS:
+            toks = slice(t0, t0 + width)
             nc.vector.tensor_copy(c_tok[:, toks, 3], planes[3][:, toks])
-            c_words = keep.tile([P, CHUNK], U32, name="c_words%d" % toks.start, align_bytes=64)
-            c_scales = keep.tile([P, CHUNK], U8, name="c_scales%d" % toks.start, align_bytes=64)
+            c_words = keep.tile([P, width], U32, name="c_words%d" % t0, align_bytes=64)
+            c_scales = keep.tile([P, width], U8, name="c_scales%d" % t0, align_bytes=64)
             nc.vector.quantize_mx(
                 out=c_words[:].bitcast(FP8X4), scales=c_scales[:], in_=c_tok[:, toks, :].rearrange("p t d -> p (t d)")
             )
-            for m0 in range(0, N // P, 2):
-                acc2 = ps_o.tile([P, 2, CHUNK], F32, name="acc2")
-                for j in range(2):
+            m0 = 0
+            for count in groups:
+                acc2 = ps_o.tile([P, count, width], F32, name="acc2")
+                for j in range(count):
                     m = m0 + j
                     nc.tensor.matmul_mx(
                         out=acc2[:, j, :],
@@ -182,9 +179,11 @@ def tile_moe_sdn_lin_gelu_kernel(
                         start=True,
                         stop=True,
                     )
-                res = keep.tile([P, 2, CHUNK], F32, name="res%d_%d" % (toks.start, m0))
-                if toks.stop == T and m0 > 0:
+                res = keep.tile([P, count, width], F32, name="res%d_%d" % (t0, m0))
+                if store_no in ON_VECTOR:
                     nc.vector.tensor_copy(res[:], acc2[:])
                 else:
                     nc.scalar.copy(res[:], acc2[:])
-                nc.sync.dma_start(out=out_view[:, m0 : m0 + 2, toks], in_=res[:])
+                nc.sync.dma_start(out=out_view[:, m0 : m0 + count, toks], in_=res[:])
+                store_no += 1
+                m0 += count

@@ -27,9 +27,11 @@ SHIFTED = 112
 BANK = 512
 HALF = T // 2
 BYTE_CUTS = ((0, C), (C, T))
-WORD_CUTS = ((0, C), (C, HALF), (HALF, T))
-CHUNKS = ((0, 256, (1, 1, 2)), (256, 256, (2, 2)), (512, 256, (2, 2)), (768, 256, (2, 2)))
-ON_VECTOR = (6, 8)
+WORD_CUTS = ((0, P), (P, HALF), (HALF, T))
+SHIFT = 16
+WARM_PASSES = 6
+CHUNKS = ((0, 128, (2, 2)), (128, 128, (4,)), (256, 256, (2, 2)), (512, 256, (2, 2)), (768, 256, (2, 2)))
+ON_VECTOR = (5, 7, 8)
 
 
 def load_scale_rows(nc, plane, rows):
@@ -58,7 +60,7 @@ def tile_moe_sdn_lin_gelu_kernel(
         gate_sb = keep.tile([P, T], F32, name="gate_sb")
         identity = keep.tile([P, P], F32, name="identity")
         staged = keep.tile([P, PACK, T], F32, name="staged")
-        planes = [keep.tile([P, T], F32, name="plane%d" % d, align_bytes=64) for d in range(PACK)]
+        planes = [keep.tile([P, 2 * T if d == 3 else T], F32, name="plane%d" % d, align_bytes=64) for d in range(PACK)]
         got_scales = [keep.tile([P, hi - lo], U8, name="got_scales%d" % lo, align_bytes=64) for lo, hi in BYTE_CUTS]
         moved_scales = [keep.tile([P, hi - lo], U8, name="moved_scales%d" % lo, align_bytes=64) for lo, hi in BYTE_CUTS]
 
@@ -73,9 +75,10 @@ def tile_moe_sdn_lin_gelu_kernel(
         def gather_scales(a):
             lo, hi = BYTE_CUTS[a]
             nc.vector.tensor_copy(got_scales[a][:], x_plane[:].indirect(listed(lo, hi)))
-            nc.sync.dma_start(
+            queue = nc.scalar if a == 0 else nc.sync
+            queue.dma_start(
                 out=moved_scales[a][:].bitcast(I32)[0:SHIFTED],
-                in_=got_scales[a][:].bitcast(I32)[SCALE_ROWS : SCALE_ROWS + SHIFTED],
+                in_=got_scales[a][:].bitcast(I32)[SHIFT:P],
             )
 
         nc.vector.memset(x_plane[:].bitcast(I32), 0)
@@ -86,12 +89,10 @@ def tile_moe_sdn_lin_gelu_kernel(
         make_identity(nc, identity[:])
 
         nc.sync.dma_start(offsets[:], offs)
-        x_rows = x_scales.bitcast(I32)
-        for q in range(P // QUADRANT):
-            nc.sync.dma_start(
-                out=x_plane[:].bitcast(I32)[QUADRANT * q : QUADRANT * q + PASSES * SCALE_ROWS],
-                in_=x_rows[:, SCALE_ROWS * q : SCALE_ROWS * (q + 1), :],
-            )
+        x_rows = x_scales.bitcast(I32).rearrange("s (q r) t -> r q s t", r=SCALE_ROWS)
+        for r in range(SCALE_ROWS):
+            queue = nc.scalar if r % 2 else nc.sync
+            queue.dma_start(out=x_plane[:].bitcast(I32)[r:P:SHIFT], in_=x_rows[r])
         nc.sync.dma_start(out=x_sb[:], in_=x_words.rearrange("s p t d -> p s (t d)").bitcast(I32))
         load_w1(0)
         load_scale_rows(nc, w1_plane, w1_scales.rearrange("e s b i -> b (e s) i"))
@@ -141,41 +142,58 @@ def tile_moe_sdn_lin_gelu_kernel(
 
         c_tok = keep.tile([P, T, PACK], BF16, name="c_tok", align_bytes=64)
 
-        for d in range(PACK):
-            scatter(d, 0, P)
-        for d in range(2):
-            scatter(d, P, HALF)
+        for lo, hi in ((0, P), (P, C), (C, HALF)):
+            for d in (2, 0, 1):
+                scatter(d, lo, hi)
+        scatter(2, HALF, T)
+        nc.scalar.copy(c_tok[:, :, 2:4], planes[2][:].unsqueeze(2).to_broadcast([P, T, 2]))
         for d in range(2):
             scatter(d, HALF, T)
             nc.scalar.copy(c_tok[:, :, d], planes[d][:])
-        scatter(2, P, HALF)
-        scatter(2, HALF, T)
-        nc.scalar.copy(c_tok[:, :, 2:4], planes[2][:].unsqueeze(2).to_broadcast([P, T, 2]))
-        scatter(3, P, HALF)
-        scatter(3, HALF, T)
+        scatter(3, 0, T)
 
+        warm = ps_h.tile([P, H], F32, name="acc")
+        last_words = c_tok[:, T - C :, :].rearrange("p t d -> p (t d)").bitcast(F32)
+        for j0 in range(0, H, P):
+            nc.tensor.transpose(warm[:, j0 : j0 + P], last_words[:, j0 : j0 + P], identity[:])
+        for rep in range(WARM_PASSES):
+            nc.tensor.matmul_mx(
+                out=warm[:],
+                lhsT=got_words[0, 0].bitcast(FP8X4),
+                lhsT_scale=got_scales[0][:, 0:P],
+                rhs=w1_sb[:, 0, 0, :].bitcast(FP4X4),
+                rhs_scale=w1_plane[:, 0, :],
+                start=True,
+                stop=True,
+            )
 
         out_view = out.rearrange("(m p) t -> p m t", p=P)
-        store_no = 0
+        c_words = keep.tile([P, T], U32, name="c_words", align_bytes=64)
+        c_scales = keep.tile([P, T], U8, name="c_scales", align_bytes=64)
         for t0, width, groups in CHUNKS:
             toks = slice(t0, t0 + width)
             nc.vector.tensor_copy(c_tok[:, toks, 3], planes[3][:, toks])
-            c_words = keep.tile([P, width], U32, name="c_words%d" % t0, align_bytes=64)
-            c_scales = keep.tile([P, width], U8, name="c_scales%d" % t0, align_bytes=64)
             nc.vector.quantize_mx(
-                out=c_words[:].bitcast(FP8X4), scales=c_scales[:], in_=c_tok[:, toks, :].rearrange("p t d -> p (t d)")
+                out=c_words[:, toks].bitcast(FP8X4),
+                scales=c_scales[:, toks],
+                in_=c_tok[:, toks, :].rearrange("p t d -> p (t d)"),
             )
+        banks = [(ps_o, "acc2")] * 4 + [(ps_t, "turned")] * 2 + [(ps_h, "acc")] * 2
+        store_no = 0
+        for t0, width, groups in CHUNKS:
+            toks = slice(t0, t0 + width)
             m0 = 0
             for count in groups:
-                acc2 = ps_o.tile([P, count, width], F32, name="acc2")
+                pool, tag = banks[store_no % len(banks)]
+                acc2 = pool.tile([P, count, width], F32, name=tag)
                 for j in range(count):
                     m = m0 + j
                     nc.tensor.matmul_mx(
                         out=acc2[:, j, :],
                         lhsT=w2_sb[:, 2 * P * m : 2 * P * (m + 1)].bitcast(FP4X4),
                         lhsT_scale=w2_plane[:, 0, P * m : P * (m + 1)],
-                        rhs=c_words[:].bitcast(FP8X4),
-                        rhs_scale=c_scales[:],
+                        rhs=c_words[:, toks].bitcast(FP8X4),
+                        rhs_scale=c_scales[:, toks],
                         start=True,
                         stop=True,
                     )

@@ -29,7 +29,7 @@ HALF = T // 2
 BYTE_CUTS = ((0, C), (C, T))
 WORD_CUTS = ((0, P), (P, HALF), (HALF, T))
 SHIFT = 16
-WARM_PASSES = 6
+WARM_PASSES = 4
 CHUNKS = ((0, 128, (2, 2)), (128, 128, (4,)), (256, 256, (2, 2)), (512, 256, (2, 2)), (768, 256, (2, 2)))
 ON_VECTOR = (5, 7, 8)
 
@@ -57,10 +57,11 @@ def tile_moe_sdn_lin_gelu_kernel(
         x_sb = keep.tile([P, PASSES, T], I32, name="x_sb", align_bytes=64)
         w1_sb = keep.tile([P, E, PASSES, 2 * H], U8, name="w1_sb", align_bytes=64)
         w2_sb = keep.tile([P, 2 * N], U8, name="w2_sb", align_bytes=64)
-        gate_sb = keep.tile([P, T], F32, name="gate_sb")
+        gate_rows = keep.tile([P, P], F32, name="gate_rows")
+        gate_cols = keep.tile([P, T // P], F32, name="gate_cols")
         identity = keep.tile([P, P], F32, name="identity")
-        staged = keep.tile([P, PACK, T], F32, name="staged")
-        planes = [keep.tile([P, 2 * T if d == 3 else T], F32, name="plane%d" % d, align_bytes=64) for d in range(PACK)]
+        staged = keep.tile([P, 2, T], F32, name="staged")
+        planes = [keep.tile([P, T], F32, name="plane%d" % u, align_bytes=64) for u in range(2)]
         got_scales = [keep.tile([P, hi - lo], U8, name="got_scales%d" % lo, align_bytes=64) for lo, hi in BYTE_CUTS]
         moved_scales = [keep.tile([P, hi - lo], U8, name="moved_scales%d" % lo, align_bytes=64) for lo, hi in BYTE_CUTS]
 
@@ -81,11 +82,12 @@ def tile_moe_sdn_lin_gelu_kernel(
                 in_=got_scales[a][:].bitcast(I32)[SHIFT:P],
             )
 
-        nc.vector.memset(x_plane[:].bitcast(I32), 0)
+        nc.gpsimd.memset(x_plane[:].bitcast(I32), 0)
         nc.vector.memset(w1_plane[:].bitcast(I32), 0)
         for moved in moved_scales:
             nc.vector.memset(moved[:].bitcast(I32), 0)
         nc.vector.memset(w2_plane[:].bitcast(I32), 0)
+        nc.gpsimd.memset(gate_rows[:], 0.0)
         make_identity(nc, identity[:])
 
         nc.sync.dma_start(offsets[:], offs)
@@ -96,10 +98,10 @@ def tile_moe_sdn_lin_gelu_kernel(
         nc.sync.dma_start(out=x_sb[:], in_=x_words.rearrange("s p t d -> p s (t d)").bitcast(I32))
         load_w1(0)
         load_scale_rows(nc, w1_plane, w1_scales.rearrange("e s b i -> b (e s) i"))
+        nc.sync.dma_start(out=gate_rows[0 : T // P, :], in_=gate[0].rearrange("(b p) -> b p", p=P))
         gather_scales(0)
         load_w1(1)
         gather_scales(1)
-        nc.sync.dma_start(out=gate_sb[:], in_=gate)
         for e in range(2, E):
             load_w1(e)
         nc.sync.dma_start(out=w2_sb[:].bitcast(I32), in_=w2_words[0].bitcast(I32))
@@ -112,6 +114,10 @@ def tile_moe_sdn_lin_gelu_kernel(
                 nc.vector.tensor_copy(words[:], x_sb[:, s, :].bitcast(U32).indirect(listed(lo, hi)))
                 for j0 in range(lo, hi, P):
                     got_words[j0, s] = words[:, j0 - lo : j0 - lo + P]
+
+        gate_ps = ps_o.tile([P, P], F32, name="acc2")
+        nc.tensor.transpose(gate_ps[:], gate_rows[:], identity[:])
+        nc.scalar.copy(gate_cols[:], gate_ps[:, 0 : T // P])
 
         for j0 in range(0, T, P):
             e = j0 // C
@@ -128,34 +134,31 @@ def tile_moe_sdn_lin_gelu_kernel(
                     start=(s == 0),
                     stop=(s == PASSES - 1),
                 )
-            h = ring.tile([P, PACK, P], F32, name="h")
-            nc.scalar.activation(h[:], acc[:].rearrange("p (q d) -> p d q", d=PACK), ACT.Gelu_apprx_tanh)
-            turned = ps_t.tile([P, PACK, P], F32, name="turned")
-            for d in range(PACK):
-                nc.tensor.transpose(turned[:, d, :], h[:, d, :], identity[:])
+            h = ring.tile([P, 2, P, 2], F32, name="h")
+            nc.scalar.activation(h[:], acc[:].rearrange("p (q u e) -> p u q e", u=2, e=2), ACT.Gelu_apprx_tanh)
+            pairs = ring.tile([P, H], BF16, name="pairs")
+            nc.scalar.activation(
+                pairs[:], h[:].rearrange("p u q e -> p (u q e)"), ACT.Copy, scale=gate_cols[:, j0 // P : j0 // P + 1]
+            )
+            turned = ps_t.tile([P, 2, P], F32, name="turned")
+            for u in range(2):
+                nc.tensor.transpose(turned[:, u, :], pairs[:].bitcast(F32)[:, u * P : (u + 1) * P], identity[:])
             nc.scalar.copy(staged[:, :, j0 : j0 + P], turned[:])
 
-        def scatter(d, lo, hi):
-            nc.vector.tensor_tensor(
-                planes[d][:].indirect(listed(lo, hi)), staged[:, d, lo:hi], gate_sb[:, lo:hi], ALU.mult
-            )
+        def scatter(u, lo, hi):
+            nc.vector.tensor_copy(planes[u][:].indirect(listed(lo, hi)), staged[:, u, lo:hi])
 
-        c_tok = keep.tile([P, T, PACK], BF16, name="c_tok", align_bytes=64)
+        for j0 in range(0, T, C):
+            for u in range(2):
+                scatter(u, j0, j0 + C)
 
-        for lo, hi in ((0, P), (P, C), (C, HALF)):
-            for d in (2, 0, 1):
-                scatter(d, lo, hi)
-        scatter(2, HALF, T)
-        nc.scalar.copy(c_tok[:, :, 2:4], planes[2][:].unsqueeze(2).to_broadcast([P, T, 2]))
-        for d in range(2):
-            scatter(d, HALF, T)
-            nc.scalar.copy(c_tok[:, :, d], planes[d][:])
-        scatter(3, 0, T)
+        c_tok = {}
+        for t0, width, groups in CHUNKS:
+            c_tok[t0] = keep.tile([P, width, 2], F32, name="c_tok%d" % t0, align_bytes=64)
+            nc.scalar.copy(c_tok[t0][:], planes[0][:, t0 : t0 + width].unsqueeze(2).to_broadcast([P, width, 2]))
 
         warm = ps_h.tile([P, H], F32, name="acc")
-        last_words = c_tok[:, T - C :, :].rearrange("p t d -> p (t d)").bitcast(F32)
-        for j0 in range(0, H, P):
-            nc.tensor.transpose(warm[:, j0 : j0 + P], last_words[:, j0 : j0 + P], identity[:])
+        nc.tensor.transpose(warm[:, 0:P], planes[0][:, 0:P], identity[:])
         for rep in range(WARM_PASSES):
             nc.tensor.matmul_mx(
                 out=warm[:],
@@ -172,11 +175,11 @@ def tile_moe_sdn_lin_gelu_kernel(
         c_scales = keep.tile([P, T], U8, name="c_scales", align_bytes=64)
         for t0, width, groups in CHUNKS:
             toks = slice(t0, t0 + width)
-            nc.vector.tensor_copy(c_tok[:, toks, 3], planes[3][:, toks])
+            nc.vector.tensor_copy(c_tok[t0][:, :, 1], planes[1][:, toks])
             nc.vector.quantize_mx(
                 out=c_words[:, toks].bitcast(FP8X4),
                 scales=c_scales[:, toks],
-                in_=c_tok[:, toks, :].rearrange("p t d -> p (t d)"),
+                in_=c_tok[t0][:].rearrange("p t u -> p (t u)").bitcast(BF16),
             )
         banks = [(ps_o, "acc2")] * 4 + [(ps_t, "turned")] * 2 + [(ps_h, "acc")] * 2
         store_no = 0

@@ -26,8 +26,8 @@ QUADRANT = 32
 SHIFTED = 112
 BANK = 512
 HALF = T // 2
-BYTE_CUTS = ((0, C), (C, T))
-WORD_CUTS = ((0, P), (P, HALF), (HALF, T))
+BYTE_CUTS = ((0, HALF), (HALF, T))
+WORD_CUTS = ((0, P), (P, C), (C, 2 * C), (2 * C, 3 * C), (3 * C, T))
 SHIFT = 16
 WARM_PASSES = 4
 CHUNKS = ((0, 128, (2, 2)), (128, 128, (4,)), (256, 256, (2, 2)), (512, 256, (2, 2)), (768, 256, (2, 2)))
@@ -95,11 +95,15 @@ def tile_moe_sdn_lin_gelu_kernel(
         for r in range(SCALE_ROWS):
             queue = nc.scalar if r % 2 else nc.sync
             queue.dma_start(out=x_plane[:].bitcast(I32)[r:P:SHIFT], in_=x_rows[r])
+        nc.sync.dma_start(out=gate_rows[0 : T // P, :], in_=gate[0].rearrange("(b p) -> b p", p=P))
         nc.sync.dma_start(out=x_sb[:], in_=x_words.rearrange("s p t d -> p s (t d)").bitcast(I32))
         load_w1(0)
         load_scale_rows(nc, w1_plane, w1_scales.rearrange("e s b i -> b (e s) i"))
-        nc.sync.dma_start(out=gate_rows[0 : T // P, :], in_=gate[0].rearrange("(b p) -> b p", p=P))
         gather_scales(0)
+        gate_ps = ps_o.tile([P, P], F32, name="acc2")
+        nc.tensor.transpose(gate_ps[:], gate_rows[:], identity[:])
+        nc.vector.tensor_copy(gate_cols[:], gate_ps[:, 0 : T // P])
+
         load_w1(1)
         gather_scales(1)
         for e in range(2, E):
@@ -115,13 +119,9 @@ def tile_moe_sdn_lin_gelu_kernel(
                 for j0 in range(lo, hi, P):
                     got_words[j0, s] = words[:, j0 - lo : j0 - lo + P]
 
-        gate_ps = ps_o.tile([P, P], F32, name="acc2")
-        nc.tensor.transpose(gate_ps[:], gate_rows[:], identity[:])
-        nc.scalar.copy(gate_cols[:], gate_ps[:, 0 : T // P])
-
         for j0 in range(0, T, P):
             e = j0 // C
-            a = min(e, 1)
+            a = j0 // HALF
             cols = slice(j0 - BYTE_CUTS[a][0], j0 - BYTE_CUTS[a][0] + P)
             acc = ps_h.tile([P, H], F32, name="acc")
             for s, scales in enumerate((got_scales, moved_scales)):
@@ -137,8 +137,8 @@ def tile_moe_sdn_lin_gelu_kernel(
             h = ring.tile([P, 2, P, 2], F32, name="h")
             nc.scalar.activation(h[:], acc[:].rearrange("p (q u e) -> p u q e", u=2, e=2), ACT.Gelu_apprx_tanh)
             pairs = ring.tile([P, H], BF16, name="pairs")
-            nc.scalar.activation(
-                pairs[:], h[:].rearrange("p u q e -> p (u q e)"), ACT.Copy, scale=gate_cols[:, j0 // P : j0 // P + 1]
+            nc.gpsimd.tensor_scalar(
+                pairs[:], h[:].rearrange("p u q e -> p (u q e)"), gate_cols[:, j0 // P : j0 // P + 1], 0.0, ALU.mult, ALU.add
             )
             turned = ps_t.tile([P, 2, P], F32, name="turned")
             for u in range(2):
@@ -148,9 +148,9 @@ def tile_moe_sdn_lin_gelu_kernel(
         def scatter(u, lo, hi):
             nc.vector.tensor_copy(planes[u][:].indirect(listed(lo, hi)), staged[:, u, lo:hi])
 
-        for j0 in range(0, T, C):
+        for lo, hi in WORD_CUTS:
             for u in range(2):
-                scatter(u, j0, j0 + C)
+                scatter(u, lo, hi)
 
         c_tok = {}
         for t0, width, groups in CHUNKS:

@@ -29,7 +29,6 @@ HALF = T // 2
 BYTE_CUTS = ((0, HALF), (HALF, T))
 WORD_CUTS = ((0, P), (P, C), (C, 2 * C), (2 * C, 3 * C), (3 * C, T))
 SHIFT = 16
-WARM_PASSES = 4
 CHUNKS = ((0, 128, (2, 2)), (128, 128, (4,)), (256, 256, (2, 2)), (512, 256, (2, 2)), (768, 256, (2, 2)))
 ON_VECTOR = (5, 7, 8)
 
@@ -156,19 +155,6 @@ def tile_moe_sdn_lin_gelu_kernel(
         for t0, width, groups in CHUNKS:
             c_tok[t0] = keep.tile([P, width, 2], F32, name="c_tok%d" % t0, align_bytes=64)
             nc.scalar.copy(c_tok[t0][:], planes[0][:, t0 : t0 + width].unsqueeze(2).to_broadcast([P, width, 2]))
-
-        warm = ps_h.tile([P, H], F32, name="acc")
-        nc.tensor.transpose(warm[:, 0:P], planes[0][:, 0:P], identity[:])
-        for rep in range(WARM_PASSES):
-            nc.tensor.matmul_mx(
-                out=warm[:],
-                lhsT=got_words[0, 0].bitcast(FP8X4),
-                lhsT_scale=got_scales[0][:, 0:P],
-                rhs=w1_sb[:, 0, 0, :].bitcast(FP4X4),
-                rhs_scale=w1_plane[:, 0, :],
-                start=True,
-                stop=True,
-            )
 
         out_view = out.rearrange("(m p) t -> p m t", p=P)
         c_words = keep.tile([P, T], U32, name="c_words", align_bytes=64)

@@ -26,11 +26,15 @@ QUADRANT = 32
 SHIFTED = 112
 BANK = 512
 HALF = T // 2
-BYTE_CUTS = ((0, HALF), (HALF, T))
+BYTE_CUTS = ((0, P), (P, HALF), (HALF, T))
+SCATTER_CUTS = ((0, P), (P, C), (C, 3 * P), (3 * P, HALF), (HALF, 3 * C), (3 * C, T))
 WORD_CUTS = ((0, P), (P, C), (C, 2 * C), (2 * C, 3 * C), (3 * C, T))
 SHIFT = 16
 CHUNKS = ((0, 128, (2, 2)), (128, 128, (4,)), (256, 256, (2, 2)), (512, 256, (2, 2)), (768, 256, (2, 2)))
 ON_VECTOR = (5, 7, 8)
+BANKS = 8
+AHEAD = 3
+GATE_STEP = 4
 
 
 def load_scale_rows(nc, plane, rows):
@@ -44,20 +48,17 @@ def tile_moe_sdn_lin_gelu_kernel(
     nc = tc.nc
     with ExitStack() as ctx:
         keep = ctx.enter_context(tc.tile_pool(name="keep", bufs=1))
-        ring = ctx.enter_context(tc.tile_pool(name="ring", bufs=3))
-        ps_h = ctx.enter_context(tc.psum_pool(name="ps_h", bufs=2))
-        ps_t = ctx.enter_context(tc.psum_pool(name="ps_t", bufs=2))
-        ps_o = ctx.enter_context(tc.psum_pool(name="ps_o", bufs=4))
+        psum = ctx.enter_context(tc.psum_pool(name="psum", bufs=1))
 
         offsets = keep.tile([P, T // LIST_ROWS], U16, name="offsets")
         x_plane = keep.tile([P, T], U8, name="x_plane", align_bytes=64)
         w1_plane = keep.tile([P, E * PASSES, H], U8, name="w1_plane", align_bytes=64)
         w2_plane = keep.tile([P, 1, N], U8, name="w2_plane", align_bytes=64)
-        x_sb = keep.tile([P, PASSES, T], I32, name="x_sb", align_bytes=64)
-        w1_sb = keep.tile([P, E, PASSES, 2 * H], U8, name="w1_sb", align_bytes=64)
         w2_sb = keep.tile([P, 2 * N], U8, name="w2_sb", align_bytes=64)
-        gate_rows = keep.tile([P, P], F32, name="gate_rows")
-        gate_cols = keep.tile([P, T // P], F32, name="gate_cols")
+        x_sb = keep.tile([P, PASSES, T], I32, name="x_sb", align_bytes=64)
+        w1_sb = [keep.tile([P, PASSES, 2 * H], U8, name="w1_sb%d" % e, align_bytes=64) for e in range(E)]
+        gate_rows = keep.tile([P, QUADRANT], F32, name="gate_rows", align_bytes=64)
+        gate_cols = keep.tile([P, QUADRANT], F32, name="gate_cols", align_bytes=64)
         identity = keep.tile([P, P], F32, name="identity")
         staged = keep.tile([P, 2, T], F32, name="staged")
         planes = [keep.tile([P, T], F32, name="plane%d" % u, align_bytes=64) for u in range(2)]
@@ -66,7 +67,7 @@ def tile_moe_sdn_lin_gelu_kernel(
 
         def load_w1(e):
             nc.sync.dma_start(
-                out=w1_sb[:, e].bitcast(I32), in_=w1_words[e].rearrange("s p b -> p s b").bitcast(I32)
+                out=w1_sb[e][:].bitcast(I32), in_=w1_words[e].rearrange("s p b -> p s b").bitcast(I32)
             )
 
         def listed(lo, hi):
@@ -75,18 +76,17 @@ def tile_moe_sdn_lin_gelu_kernel(
         def gather_scales(a):
             lo, hi = BYTE_CUTS[a]
             nc.vector.tensor_copy(got_scales[a][:], x_plane[:].indirect(listed(lo, hi)))
-            queue = nc.scalar if a == 0 else nc.sync
-            queue.dma_start(
+            nc.sync.dma_start(
                 out=moved_scales[a][:].bitcast(I32)[0:SHIFTED],
                 in_=got_scales[a][:].bitcast(I32)[SHIFT:P],
             )
 
         nc.gpsimd.memset(x_plane[:].bitcast(I32), 0)
+        nc.gpsimd.memset(gate_rows[:], 0.0)
         nc.vector.memset(w1_plane[:].bitcast(I32), 0)
         for moved in moved_scales:
             nc.vector.memset(moved[:].bitcast(I32), 0)
         nc.vector.memset(w2_plane[:].bitcast(I32), 0)
-        nc.gpsimd.memset(gate_rows[:], 0.0)
         make_identity(nc, identity[:])
 
         nc.sync.dma_start(offsets[:], offs)
@@ -94,25 +94,22 @@ def tile_moe_sdn_lin_gelu_kernel(
         for r in range(SCALE_ROWS):
             queue = nc.scalar if r % 2 else nc.sync
             queue.dma_start(out=x_plane[:].bitcast(I32)[r:P:SHIFT], in_=x_rows[r])
-        nc.sync.dma_start(out=gate_rows[0 : T // P, :], in_=gate[0].rearrange("(b p) -> b p", p=P))
+        nc.scalar.dma_start(out=gate_rows[0:P:GATE_STEP, :], in_=gate[0].rearrange("(b a i) -> a b i", a=P // QUADRANT, i=QUADRANT))
         nc.sync.dma_start(out=x_sb[:], in_=x_words.rearrange("s p t d -> p s (t d)").bitcast(I32))
         load_w1(0)
         load_scale_rows(nc, w1_plane, w1_scales.rearrange("e s b i -> b (e s) i"))
+        nc.vector.transpose(gate_cols[:], gate_rows[:])
         gather_scales(0)
-        gate_ps = ps_o.tile([P, P], F32, name="acc2")
-        nc.tensor.transpose(gate_ps[:], gate_rows[:], identity[:])
-        nc.vector.tensor_copy(gate_cols[:], gate_ps[:, 0 : T // P])
 
-        load_w1(1)
         gather_scales(1)
+        load_w1(1)
+        gather_scales(2)
         for e in range(2, E):
             load_w1(e)
-        nc.sync.dma_start(out=w2_sb[:].bitcast(I32), in_=w2_words[0].bitcast(I32))
-        load_scale_rows(nc, w2_plane, w2_scales.rearrange("s b n -> b s n"))
 
         got_words = {}
         for lo, hi in WORD_CUTS:
-            for s in range(PASSES):
+            for s in (1, 0):
                 words = keep.tile([P, hi - lo], U32, name="got_words%d_%d" % (lo, s), align_bytes=64)
                 nc.vector.tensor_copy(words[:], x_sb[:, s, :].bitcast(U32).indirect(listed(lo, hi)))
                 for j0 in range(lo, hi, P):
@@ -120,34 +117,38 @@ def tile_moe_sdn_lin_gelu_kernel(
 
         for j0 in range(0, T, P):
             e = j0 // C
-            a = j0 // HALF
+            b = j0 // P
+            a = [j0 < hi for lo, hi in BYTE_CUTS].index(True)
             cols = slice(j0 - BYTE_CUTS[a][0], j0 - BYTE_CUTS[a][0] + P)
-            acc = ps_h.tile([P, H], F32, name="acc")
-            for s, scales in enumerate((got_scales, moved_scales)):
+            acc = psum.tile([P, H], F32, name="bank%d" % b)
+            for s, scales in ((1, moved_scales), (0, got_scales)):
                 nc.tensor.matmul_mx(
                     out=acc[:],
                     lhsT=got_words[j0, s].bitcast(FP8X4),
                     lhsT_scale=scales[a][:, cols],
-                    rhs=w1_sb[:, e, s, :].bitcast(FP4X4),
+                    rhs=w1_sb[e][:, s, :].bitcast(FP4X4),
                     rhs_scale=w1_plane[:, e * PASSES + s, :],
-                    start=(s == 0),
-                    stop=(s == PASSES - 1),
+                    start=(s == 1),
+                    stop=(s == 0),
                 )
-            h = ring.tile([P, 2, P, 2], F32, name="h")
+            h = keep.tile([P, 2, P, 2], F32, name="h%d" % b, align_bytes=64)
             nc.scalar.activation(h[:], acc[:].rearrange("p (q u e) -> p u q e", u=2, e=2), ACT.Gelu_apprx_tanh)
-            pairs = ring.tile([P, H], BF16, name="pairs")
+            pairs = keep.tile([P, H], BF16, name="pairs%d" % b)
             nc.gpsimd.tensor_scalar(
-                pairs[:], h[:].rearrange("p u q e -> p (u q e)"), gate_cols[:, j0 // P : j0 // P + 1], 0.0, ALU.mult, ALU.add
+                pairs[:], h[:].rearrange("p u q e -> p (u q e)"), gate_cols[:, GATE_STEP * b : GATE_STEP * b + 1], 0.0, ALU.mult, ALU.add
             )
-            turned = ps_t.tile([P, 2, P], F32, name="turned")
+            turned = psum.tile([P, 2, P], F32, name="bank%d" % ((b + AHEAD) % BANKS))
             for u in range(2):
                 nc.tensor.transpose(turned[:, u, :], pairs[:].bitcast(F32)[:, u * P : (u + 1) * P], identity[:])
             nc.scalar.copy(staged[:, :, j0 : j0 + P], turned[:])
 
+        nc.sync.dma_start(out=w2_sb[:].bitcast(I32), in_=w2_words[0].bitcast(I32))
+        load_scale_rows(nc, w2_plane, w2_scales.rearrange("s b n -> b s n"))
+
         def scatter(u, lo, hi):
             nc.vector.tensor_copy(planes[u][:].indirect(listed(lo, hi)), staged[:, u, lo:hi])
 
-        for lo, hi in WORD_CUTS:
+        for lo, hi in SCATTER_CUTS:
             for u in range(2):
                 scatter(u, lo, hi)
 
@@ -167,14 +168,12 @@ def tile_moe_sdn_lin_gelu_kernel(
                 scales=c_scales[:, toks],
                 in_=c_tok[t0][:].rearrange("p t u -> p (t u)").bitcast(BF16),
             )
-        banks = [(ps_o, "acc2")] * 4 + [(ps_t, "turned")] * 2 + [(ps_h, "acc")] * 2
         store_no = 0
         for t0, width, groups in CHUNKS:
             toks = slice(t0, t0 + width)
             m0 = 0
             for count in groups:
-                pool, tag = banks[store_no % len(banks)]
-                acc2 = pool.tile([P, count, width], F32, name=tag)
+                acc2 = psum.tile([P, count, width], F32, name="bank%d" % (store_no % BANKS))
                 for j in range(count):
                     m = m0 + j
                     nc.tensor.matmul_mx(

@@ -33,8 +33,8 @@ SHIFT = 16
 CHUNKS = ((0, 128, (2, 2)), (128, 128, (4,)), (256, 256, (2, 2)), (512, 256, (2, 2)), (768, 256, (2, 2)))
 ON_VECTOR = (5, 7, 8)
 BANKS = 8
-AHEAD = 3
 GATE_STEP = 4
+WARM_PASSES = 4
 
 
 def load_scale_rows(nc, plane, rows):
@@ -52,11 +52,12 @@ def tile_moe_sdn_lin_gelu_kernel(
 
         offsets = keep.tile([P, T // LIST_ROWS], U16, name="offsets")
         x_plane = keep.tile([P, T], U8, name="x_plane", align_bytes=64)
-        w1_plane = keep.tile([P, E * PASSES, H], U8, name="w1_plane", align_bytes=64)
+        w1_planes = [keep.tile([P, E, H], U8, name="w1_plane%d" % g, align_bytes=64) for g in range(2)]
         w2_plane = keep.tile([P, 1, N], U8, name="w2_plane", align_bytes=64)
         w2_sb = keep.tile([P, 2 * N], U8, name="w2_sb", align_bytes=64)
+        c_words = keep.tile([P, T], U32, name="c_words", align_bytes=64)
         x_sb = keep.tile([P, PASSES, T], I32, name="x_sb", align_bytes=64)
-        w1_sb = [keep.tile([P, PASSES, 2 * H], U8, name="w1_sb%d" % e, align_bytes=64) for e in range(E)]
+        w1_sb = [keep.tile([P, PASSES, 2 * H], U8, name="w1_sb%d" % e, align_bytes=64) for e in range(2)]
         gate_rows = keep.tile([P, QUADRANT], F32, name="gate_rows", align_bytes=64)
         gate_cols = keep.tile([P, QUADRANT], F32, name="gate_cols", align_bytes=64)
         identity = keep.tile([P, P], F32, name="identity")
@@ -76,17 +77,21 @@ def tile_moe_sdn_lin_gelu_kernel(
         def gather_scales(a):
             lo, hi = BYTE_CUTS[a]
             nc.vector.tensor_copy(got_scales[a][:], x_plane[:].indirect(listed(lo, hi)))
-            nc.sync.dma_start(
+            queue = nc.scalar if a == 0 else nc.sync
+            queue.dma_start(
                 out=moved_scales[a][:].bitcast(I32)[0:SHIFTED],
                 in_=got_scales[a][:].bitcast(I32)[SHIFT:P],
             )
 
         nc.gpsimd.memset(x_plane[:].bitcast(I32), 0)
         nc.gpsimd.memset(gate_rows[:], 0.0)
-        nc.vector.memset(w1_plane[:].bitcast(I32), 0)
+        nc.vector.memset(w1_planes[0][:].bitcast(I32), 0)
         for moved in moved_scales:
             nc.vector.memset(moved[:].bitcast(I32), 0)
+        nc.vector.memset(w1_planes[1][:].bitcast(I32), 0)
         nc.vector.memset(w2_plane[:].bitcast(I32), 0)
+        nc.gpsimd.memset(w2_sb[:].bitcast(I32), 0)
+        nc.gpsimd.memset(c_words[:, 0:P], 0)
         make_identity(nc, identity[:])
 
         nc.sync.dma_start(offsets[:], offs)
@@ -97,19 +102,29 @@ def tile_moe_sdn_lin_gelu_kernel(
         nc.scalar.dma_start(out=gate_rows[0:P:GATE_STEP, :], in_=gate[0].rearrange("(b a i) -> a b i", a=P // QUADRANT, i=QUADRANT))
         nc.sync.dma_start(out=x_sb[:], in_=x_words.rearrange("s p t d -> p s (t d)").bitcast(I32))
         load_w1(0)
-        load_scale_rows(nc, w1_plane, w1_scales.rearrange("e s b i -> b (e s) i"))
+        load_scale_rows(nc, w1_planes[0], w1_scales[0:2].rearrange("e s b i -> b (e s) i"))
         nc.vector.transpose(gate_cols[:], gate_rows[:])
         gather_scales(0)
+        warm = psum.tile([P, N], F32, name="bank%d" % (BANKS - 1))
+        for i in range(WARM_PASSES):
+            nc.tensor.matmul_mx(
+                out=warm[:],
+                lhsT=c_words[:, 0:P].bitcast(FP8X4),
+                lhsT_scale=got_scales[0][:, 0:P],
+                rhs=w2_sb[:].bitcast(FP4X4),
+                rhs_scale=w2_plane[:, 0, :],
+                start=True,
+                stop=True,
+            )
 
         gather_scales(1)
         load_w1(1)
         gather_scales(2)
-        for e in range(2, E):
-            load_w1(e)
+        load_scale_rows(nc, w1_planes[1], w1_scales[2:4].rearrange("e s b i -> b (e s) i"))
 
         got_words = {}
         for lo, hi in WORD_CUTS:
-            for s in (1, 0):
+            for s in range(PASSES):
                 words = keep.tile([P, hi - lo], U32, name="got_words%d_%d" % (lo, s), align_bytes=64)
                 nc.vector.tensor_copy(words[:], x_sb[:, s, :].bitcast(U32).indirect(listed(lo, hi)))
                 for j0 in range(lo, hi, P):
@@ -119,17 +134,20 @@ def tile_moe_sdn_lin_gelu_kernel(
             e = j0 // C
             b = j0 // P
             a = [j0 < hi for lo, hi in BYTE_CUTS].index(True)
+            if e >= 2 and j0 % C == 0:
+                w1_sb.append(keep.tile([P, PASSES, 2 * H], U8, name="h%d" % (e - 2), align_bytes=64))
+                load_w1(e)
             cols = slice(j0 - BYTE_CUTS[a][0], j0 - BYTE_CUTS[a][0] + P)
             acc = psum.tile([P, H], F32, name="bank%d" % b)
-            for s, scales in ((1, moved_scales), (0, got_scales)):
+            for s, scales in enumerate((got_scales, moved_scales)):
                 nc.tensor.matmul_mx(
                     out=acc[:],
                     lhsT=got_words[j0, s].bitcast(FP8X4),
                     lhsT_scale=scales[a][:, cols],
                     rhs=w1_sb[e][:, s, :].bitcast(FP4X4),
-                    rhs_scale=w1_plane[:, e * PASSES + s, :],
-                    start=(s == 1),
-                    stop=(s == 0),
+                    rhs_scale=w1_planes[e // 2][:, e % 2 * PASSES + s, :],
+                    start=(s == 0),
+                    stop=(s == PASSES - 1),
                 )
             h = keep.tile([P, 2, P, 2], F32, name="h%d" % b, align_bytes=64)
             nc.scalar.activation(h[:], acc[:].rearrange("p (q u e) -> p u q e", u=2, e=2), ACT.Gelu_apprx_tanh)
@@ -137,7 +155,7 @@ def tile_moe_sdn_lin_gelu_kernel(
             nc.gpsimd.tensor_scalar(
                 pairs[:], h[:].rearrange("p u q e -> p (u q e)"), gate_cols[:, GATE_STEP * b : GATE_STEP * b + 1], 0.0, ALU.mult, ALU.add
             )
-            turned = psum.tile([P, 2, P], F32, name="bank%d" % ((b + AHEAD) % BANKS))
+            turned = psum.tile([P, 2, P], F32, name="bank%d" % b)
             for u in range(2):
                 nc.tensor.transpose(turned[:, u, :], pairs[:].bitcast(F32)[:, u * P : (u + 1) * P], identity[:])
             nc.scalar.copy(staged[:, :, j0 : j0 + P], turned[:])
@@ -158,7 +176,6 @@ def tile_moe_sdn_lin_gelu_kernel(
             nc.scalar.copy(c_tok[t0][:], planes[0][:, t0 : t0 + width].unsqueeze(2).to_broadcast([P, width, 2]))
 
         out_view = out.rearrange("(m p) t -> p m t", p=P)
-        c_words = keep.tile([P, T], U32, name="c_words", align_bytes=64)
         c_scales = keep.tile([P, T], U8, name="c_scales", align_bytes=64)
         for t0, width, groups in CHUNKS:
             toks = slice(t0, t0 + width)

@@ -27,11 +27,11 @@ SHIFTED = 112
 BANK = 512
 HALF = T // 2
 BYTE_CUTS = ((0, P), (P, HALF), (HALF, T))
-SCATTER_CUTS = ((0, P), (P, C), (C, 3 * P), (3 * P, HALF), (HALF, 3 * C), (3 * C, T))
+SCATTERS = tuple((u, lo, hi) for lo, hi in ((0, P), (P, C), (C, 3 * P), (3 * P, HALF), (HALF, 3 * C), (3 * C, T)) for u in range(2))
 WORD_CUTS = ((0, P), (P, C), (C, 2 * C), (2 * C, 3 * C), (3 * C, T))
 SHIFT = 16
 CHUNKS = ((0, 128, (2, 2)), (128, 128, (4,)), (256, 256, (2, 2)), (512, 256, (2, 2)), (768, 256, (2, 2)))
-ON_VECTOR = (5, 7, 8)
+ON_VECTOR = (4, 6, 8)
 BANKS = 8
 GATE_STEP = 4
 WARM_PASSES = 4
@@ -90,8 +90,8 @@ def tile_moe_sdn_lin_gelu_kernel(
             nc.vector.memset(moved[:].bitcast(I32), 0)
         nc.vector.memset(w1_planes[1][:].bitcast(I32), 0)
         nc.vector.memset(w2_plane[:].bitcast(I32), 0)
-        nc.gpsimd.memset(w2_sb[:].bitcast(I32), 0)
-        nc.gpsimd.memset(c_words[:, 0:P], 0)
+        nc.vector.memset(w2_sb[:].bitcast(I32), 0)
+        nc.vector.memset(c_words[:, T - P : T].bitcast(I32), 0)
         make_identity(nc, identity[:])
 
         nc.sync.dma_start(offsets[:], offs)
@@ -109,7 +109,7 @@ def tile_moe_sdn_lin_gelu_kernel(
         for i in range(WARM_PASSES):
             nc.tensor.matmul_mx(
                 out=warm[:],
-                lhsT=c_words[:, 0:P].bitcast(FP8X4),
+                lhsT=c_words[:, T - P : T].bitcast(FP8X4),
                 lhsT_scale=got_scales[0][:, 0:P],
                 rhs=w2_sb[:].bitcast(FP4X4),
                 rhs_scale=w2_plane[:, 0, :],
@@ -166,9 +166,8 @@ def tile_moe_sdn_lin_gelu_kernel(
         def scatter(u, lo, hi):
             nc.vector.tensor_copy(planes[u][:].indirect(listed(lo, hi)), staged[:, u, lo:hi])
 
-        for lo, hi in SCATTER_CUTS:
-            for u in range(2):
-                scatter(u, lo, hi)
+        for u, lo, hi in SCATTERS:
+            scatter(u, lo, hi)
 
         c_tok = {}
         for t0, width, groups in CHUNKS:
@@ -177,20 +176,25 @@ def tile_moe_sdn_lin_gelu_kernel(
 
         out_view = out.rearrange("(m p) t -> p m t", p=P)
         c_scales = keep.tile([P, T], U8, name="c_scales", align_bytes=64)
-        for t0, width, groups in CHUNKS:
+
+        def weave(t0, width):
+            nc.vector.tensor_copy(c_tok[t0][:, :, 1], planes[1][:, t0 : t0 + width])
+
+        def quantise(t0, width):
             toks = slice(t0, t0 + width)
-            nc.vector.tensor_copy(c_tok[t0][:, :, 1], planes[1][:, toks])
             nc.vector.quantize_mx(
                 out=c_words[:, toks].bitcast(FP8X4),
                 scales=c_scales[:, toks],
                 in_=c_tok[t0][:].rearrange("p t u -> p (t u)").bitcast(BF16),
             )
-        store_no = 0
-        for t0, width, groups in CHUNKS:
+
+        stores = []
+
+        def project(t0, width, groups):
             toks = slice(t0, t0 + width)
             m0 = 0
             for count in groups:
-                acc2 = psum.tile([P, count, width], F32, name="bank%d" % (store_no % BANKS))
+                acc2 = psum.tile([P, count, width], F32, name="bank%d" % (len(stores) % BANKS))
                 for j in range(count):
                     m = m0 + j
                     nc.tensor.matmul_mx(
@@ -203,10 +207,19 @@ def tile_moe_sdn_lin_gelu_kernel(
                         stop=True,
                     )
                 res = keep.tile([P, count, width], F32, name="res%d_%d" % (t0, m0))
-                if store_no in ON_VECTOR:
+                if len(stores) in ON_VECTOR:
                     nc.vector.tensor_copy(res[:], acc2[:])
                 else:
                     nc.scalar.copy(res[:], acc2[:])
                 nc.sync.dma_start(out=out_view[:, m0 : m0 + count, toks], in_=res[:])
-                store_no += 1
+                stores.append(res)
                 m0 += count
+
+        for first, second in ((0, 1), (2, 2), (3, 4)):
+            for i in range(first, second + 1):
+                weave(*CHUNKS[i][:2])
+            for i in range(first, second + 1):
+                quantise(*CHUNKS[i][:2])
+        for chunk in CHUNKS[:3]:
+            project(*chunk)
+        project(HALF, HALF, (1, 1, 1, 1))

@@ -34,7 +34,6 @@ CHUNKS = ((0, 128, (2, 2)), (128, 128, (4,)), (256, 256, (2, 2)), (512, 256, (2,
 ON_VECTOR = (4, 6, 8)
 BANKS = 8
 GATE_STEP = 4
-WARM_PASSES = 4
 
 
 def load_scale_rows(nc, plane, rows):
@@ -90,8 +89,6 @@ def tile_moe_sdn_lin_gelu_kernel(
             nc.vector.memset(moved[:].bitcast(I32), 0)
         nc.vector.memset(w1_planes[1][:].bitcast(I32), 0)
         nc.vector.memset(w2_plane[:].bitcast(I32), 0)
-        nc.vector.memset(w2_sb[:].bitcast(I32), 0)
-        nc.vector.memset(c_words[:, T - P : T].bitcast(I32), 0)
         make_identity(nc, identity[:])
 
         nc.sync.dma_start(offsets[:], offs)
@@ -105,18 +102,6 @@ def tile_moe_sdn_lin_gelu_kernel(
         load_scale_rows(nc, w1_planes[0], w1_scales[0:2].rearrange("e s b i -> b (e s) i"))
         nc.vector.transpose(gate_cols[:], gate_rows[:])
         gather_scales(0)
-        warm = psum.tile([P, N], F32, name="bank%d" % (BANKS - 1))
-        for i in range(WARM_PASSES):
-            nc.tensor.matmul_mx(
-                out=warm[:],
-                lhsT=c_words[:, T - P : T].bitcast(FP8X4),
-                lhsT_scale=got_scales[0][:, 0:P],
-                rhs=w2_sb[:].bitcast(FP4X4),
-                rhs_scale=w2_plane[:, 0, :],
-                start=True,
-                stop=True,
-            )
-
         gather_scales(1)
         load_w1(1)
         gather_scales(2)

@@ -21,24 +21,29 @@ P = 128
 PACK = 4
 PASSES = K // (P * PACK)
 LIST_ROWS = 16
-SCALE_ROWS = 4
 QUADRANT = 32
-SHIFTED = 112
-BANK = 512
-HALF = T // 2
-BYTE_CUTS = ((0, P), (P, HALF), (HALF, T))
-SCATTERS = tuple((u, lo, hi) for lo, hi in ((0, P), (P, C), (C, 3 * P), (3 * P, HALF), (HALF, 3 * C), (3 * C, T)) for u in range(2))
-WORD_CUTS = ((0, P), (P, C), (C, 2 * C), (2 * C, 3 * C), (3 * C, T))
+QUADRANTS = P // QUADRANT
+SCALE_ROWS = 4
 SHIFT = 16
-CHUNKS = ((0, 128, (2, 2)), (128, 128, (4,)), (256, 256, (2, 2)), (512, 256, (2, 2)), (768, 256, (2, 2)))
-ON_VECTOR = (4, 6, 8)
+GATE_STEP = QUADRANT // (T // P)
 BANKS = 8
-GATE_STEP = 4
+EARLY_EXPERTS = E // 2
+MIDDLE = T // 2
+
+BYTE_CUTS = ((0, P), (P, MIDDLE), (MIDDLE, T))
+WORD_CUTS = ((0, P), (P, C), (C, 2 * C), (2 * C, 3 * C), (3 * C, T))
+SCATTER_CUTS = ((0, P), (P, C), (C, 3 * P), (3 * P, MIDDLE), (MIDDLE, 3 * C), (3 * C, T))
+QUANTISE_RUNS = (((0, P), (P, P)), ((C, C),), ((MIDDLE, C), (3 * C, C)))
+STORES = ((0, (P,), 2), (P, (P, C), 1), (MIDDLE, (MIDDLE,), 1))
+ON_VECTOR = (5, 7, 9)
 
 
 def load_scale_rows(nc, plane, rows):
     for r in range(SCALE_ROWS):
-        nc.sync.dma_start(out=plane[:].bitcast(I32)[r:P:QUADRANT], in_=rows.bitcast(I32)[r:16:SCALE_ROWS])
+        nc.sync.dma_start(
+            out=plane[:].bitcast(I32)[r:P:QUADRANT],
+            in_=rows.bitcast(I32)[r : QUADRANTS * SCALE_ROWS : SCALE_ROWS],
+        )
 
 
 def tile_moe_sdn_lin_gelu_kernel(
@@ -51,17 +56,20 @@ def tile_moe_sdn_lin_gelu_kernel(
 
         offsets = keep.tile([P, T // LIST_ROWS], U16, name="offsets")
         x_plane = keep.tile([P, T], U8, name="x_plane", align_bytes=64)
-        w1_planes = [keep.tile([P, E, H], U8, name="w1_plane%d" % g, align_bytes=64) for g in range(2)]
+        w1_planes = [
+            keep.tile([P, EARLY_EXPERTS * PASSES, H], U8, name="w1_plane%d" % g, align_bytes=64)
+            for g in range(E // EARLY_EXPERTS)
+        ]
         w2_plane = keep.tile([P, 1, N], U8, name="w2_plane", align_bytes=64)
         w2_sb = keep.tile([P, 2 * N], U8, name="w2_sb", align_bytes=64)
         c_words = keep.tile([P, T], U32, name="c_words", align_bytes=64)
         x_sb = keep.tile([P, PASSES, T], I32, name="x_sb", align_bytes=64)
-        w1_sb = [keep.tile([P, PASSES, 2 * H], U8, name="w1_sb%d" % e, align_bytes=64) for e in range(2)]
+        w1_sb = [keep.tile([P, PASSES, 2 * H], U8, name="w1_sb%d" % e, align_bytes=64) for e in range(EARLY_EXPERTS)]
         gate_rows = keep.tile([P, QUADRANT], F32, name="gate_rows", align_bytes=64)
         gate_cols = keep.tile([P, QUADRANT], F32, name="gate_cols", align_bytes=64)
         identity = keep.tile([P, P], F32, name="identity")
         staged = keep.tile([P, 2, T], F32, name="staged")
-        planes = [keep.tile([P, T], F32, name="plane%d" % u, align_bytes=64) for u in range(2)]
+        halves = [keep.tile([P, T], F32, name="plane%d" % u, align_bytes=64) for u in range(2)]
         got_scales = [keep.tile([P, hi - lo], U8, name="got_scales%d" % lo, align_bytes=64) for lo, hi in BYTE_CUTS]
         moved_scales = [keep.tile([P, hi - lo], U8, name="moved_scales%d" % lo, align_bytes=64) for lo, hi in BYTE_CUTS]
 
@@ -69,6 +77,10 @@ def tile_moe_sdn_lin_gelu_kernel(
             nc.sync.dma_start(
                 out=w1_sb[e][:].bitcast(I32), in_=w1_words[e].rearrange("s p b -> p s b").bitcast(I32)
             )
+
+        def load_w1_scales(g):
+            experts = w1_scales[g * EARLY_EXPERTS : (g + 1) * EARLY_EXPERTS]
+            load_scale_rows(nc, w1_planes[g], experts.rearrange("e s b i -> b (e s) i"))
 
         def listed(lo, hi):
             return offsets[:, lo // LIST_ROWS : hi // LIST_ROWS]
@@ -78,7 +90,7 @@ def tile_moe_sdn_lin_gelu_kernel(
             nc.vector.tensor_copy(got_scales[a][:], x_plane[:].indirect(listed(lo, hi)))
             queue = nc.scalar if a == 0 else nc.sync
             queue.dma_start(
-                out=moved_scales[a][:].bitcast(I32)[0:SHIFTED],
+                out=moved_scales[a][:].bitcast(I32)[0 : P - SHIFT],
                 in_=got_scales[a][:].bitcast(I32)[SHIFT:P],
             )
 
@@ -96,16 +108,18 @@ def tile_moe_sdn_lin_gelu_kernel(
         for r in range(SCALE_ROWS):
             queue = nc.scalar if r % 2 else nc.sync
             queue.dma_start(out=x_plane[:].bitcast(I32)[r:P:SHIFT], in_=x_rows[r])
-        nc.scalar.dma_start(out=gate_rows[0:P:GATE_STEP, :], in_=gate[0].rearrange("(b a i) -> a b i", a=P // QUADRANT, i=QUADRANT))
+        nc.scalar.dma_start(
+            out=gate_rows[0:P:GATE_STEP, :], in_=gate[0].rearrange("(b a i) -> a b i", a=QUADRANTS, i=QUADRANT)
+        )
         nc.sync.dma_start(out=x_sb[:], in_=x_words.rearrange("s p t d -> p s (t d)").bitcast(I32))
         load_w1(0)
-        load_scale_rows(nc, w1_planes[0], w1_scales[0:2].rearrange("e s b i -> b (e s) i"))
+        load_w1_scales(0)
         nc.vector.transpose(gate_cols[:], gate_rows[:])
         gather_scales(0)
         gather_scales(1)
         load_w1(1)
         gather_scales(2)
-        load_scale_rows(nc, w1_planes[1], w1_scales[2:4].rearrange("e s b i -> b (e s) i"))
+        load_w1_scales(1)
 
         got_words = {}
         for lo, hi in WORD_CUTS:
@@ -119,8 +133,8 @@ def tile_moe_sdn_lin_gelu_kernel(
             e = j0 // C
             b = j0 // P
             a = [j0 < hi for lo, hi in BYTE_CUTS].index(True)
-            if e >= 2 and j0 % C == 0:
-                w1_sb.append(keep.tile([P, PASSES, 2 * H], U8, name="h%d" % (e - 2), align_bytes=64))
+            if e >= EARLY_EXPERTS and j0 % C == 0:
+                w1_sb.append(keep.tile([P, PASSES, 2 * H], U8, name="h%d" % (e - EARLY_EXPERTS), align_bytes=64))
                 load_w1(e)
             cols = slice(j0 - BYTE_CUTS[a][0], j0 - BYTE_CUTS[a][0] + P)
             acc = psum.tile([P, H], F32, name="bank%d" % b)
@@ -130,16 +144,15 @@ def tile_moe_sdn_lin_gelu_kernel(
                     lhsT=got_words[j0, s].bitcast(FP8X4),
                     lhsT_scale=scales[a][:, cols],
                     rhs=w1_sb[e][:, s, :].bitcast(FP4X4),
-                    rhs_scale=w1_planes[e // 2][:, e % 2 * PASSES + s, :],
+                    rhs_scale=w1_planes[e // EARLY_EXPERTS][:, e % EARLY_EXPERTS * PASSES + s, :],
                     start=(s == 0),
                     stop=(s == PASSES - 1),
                 )
             h = keep.tile([P, 2, P, 2], F32, name="h%d" % b, align_bytes=64)
-            nc.scalar.activation(h[:], acc[:].rearrange("p (q u e) -> p u q e", u=2, e=2), ACT.Gelu_apprx_tanh)
+            nc.scalar.activation(h[:], acc[:].rearrange("p (q u d) -> p u q d", u=2, d=2), ACT.Gelu_apprx_tanh)
             pairs = keep.tile([P, H], BF16, name="pairs%d" % b)
-            nc.gpsimd.tensor_scalar(
-                pairs[:], h[:].rearrange("p u q e -> p (u q e)"), gate_cols[:, GATE_STEP * b : GATE_STEP * b + 1], 0.0, ALU.mult, ALU.add
-            )
+            weight = gate_cols[:, GATE_STEP * b : GATE_STEP * b + 1]
+            nc.gpsimd.tensor_scalar(pairs[:], h[:].rearrange("p u q d -> p (u q d)"), weight, 0.0, ALU.mult, ALU.add)
             turned = psum.tile([P, 2, P], F32, name="bank%d" % b)
             for u in range(2):
                 nc.tensor.transpose(turned[:, u, :], pairs[:].bitcast(F32)[:, u * P : (u + 1) * P], identity[:])
@@ -148,63 +161,51 @@ def tile_moe_sdn_lin_gelu_kernel(
         nc.sync.dma_start(out=w2_sb[:].bitcast(I32), in_=w2_words[0].bitcast(I32))
         load_scale_rows(nc, w2_plane, w2_scales.rearrange("s b n -> b s n"))
 
-        def scatter(u, lo, hi):
-            nc.vector.tensor_copy(planes[u][:].indirect(listed(lo, hi)), staged[:, u, lo:hi])
+        for lo, hi in SCATTER_CUTS:
+            for u in range(2):
+                nc.vector.tensor_copy(halves[u][:].indirect(listed(lo, hi)), staged[:, u, lo:hi])
 
-        for u, lo, hi in SCATTERS:
-            scatter(u, lo, hi)
+        woven = {}
+        for run in QUANTISE_RUNS:
+            for t0, width in run:
+                woven[t0] = keep.tile([P, width, 2], F32, name="c_tok%d" % t0, align_bytes=64)
+                nc.scalar.copy(woven[t0][:], halves[0][:, t0 : t0 + width].unsqueeze(2).to_broadcast([P, width, 2]))
 
-        c_tok = {}
-        for t0, width, groups in CHUNKS:
-            c_tok[t0] = keep.tile([P, width, 2], F32, name="c_tok%d" % t0, align_bytes=64)
-            nc.scalar.copy(c_tok[t0][:], planes[0][:, t0 : t0 + width].unsqueeze(2).to_broadcast([P, width, 2]))
+        c_scales = keep.tile([P, T], U8, name="c_scales", align_bytes=64)
+        for run in QUANTISE_RUNS:
+            for t0, width in run:
+                nc.vector.tensor_copy(woven[t0][:, :, 1], halves[1][:, t0 : t0 + width])
+            for t0, width in run:
+                nc.vector.quantize_mx(
+                    out=c_words[:, t0 : t0 + width].bitcast(FP8X4),
+                    scales=c_scales[:, t0 : t0 + width],
+                    in_=woven[t0][:].rearrange("p t u -> p (t u)").bitcast(BF16),
+                )
 
         out_view = out.rearrange("(m p) t -> p m t", p=P)
-        c_scales = keep.tile([P, T], U8, name="c_scales", align_bytes=64)
-
-        def weave(t0, width):
-            nc.vector.tensor_copy(c_tok[t0][:, :, 1], planes[1][:, t0 : t0 + width])
-
-        def quantise(t0, width):
-            toks = slice(t0, t0 + width)
-            nc.vector.quantize_mx(
-                out=c_words[:, toks].bitcast(FP8X4),
-                scales=c_scales[:, toks],
-                in_=c_tok[t0][:].rearrange("p t u -> p (t u)").bitcast(BF16),
-            )
-
-        stores = []
-
-        def project(t0, width, groups):
-            toks = slice(t0, t0 + width)
-            m0 = 0
-            for count in groups:
-                acc2 = psum.tile([P, count, width], F32, name="bank%d" % (len(stores) % BANKS))
+        store_no = 0
+        for first, widths, count in STORES:
+            span = sum(widths)
+            for m0 in range(0, N // P, count):
+                acc2 = psum.tile([P, count, span], F32, name="bank%d" % (store_no % BANKS))
                 for j in range(count):
                     m = m0 + j
-                    nc.tensor.matmul_mx(
-                        out=acc2[:, j, :],
-                        lhsT=w2_sb[:, 2 * P * m : 2 * P * (m + 1)].bitcast(FP4X4),
-                        lhsT_scale=w2_plane[:, 0, P * m : P * (m + 1)],
-                        rhs=c_words[:, toks].bitcast(FP8X4),
-                        rhs_scale=c_scales[:, toks],
-                        start=True,
-                        stop=True,
-                    )
-                res = keep.tile([P, count, width], F32, name="res%d_%d" % (t0, m0))
-                if len(stores) in ON_VECTOR:
+                    t0 = first
+                    for width in widths:
+                        nc.tensor.matmul_mx(
+                            out=acc2[:, j, t0 - first : t0 - first + width],
+                            lhsT=w2_sb[:, 2 * P * m : 2 * P * (m + 1)].bitcast(FP4X4),
+                            lhsT_scale=w2_plane[:, 0, P * m : P * (m + 1)],
+                            rhs=c_words[:, t0 : t0 + width].bitcast(FP8X4),
+                            rhs_scale=c_scales[:, t0 : t0 + width],
+                            start=True,
+                            stop=True,
+                        )
+                        t0 += width
+                res = keep.tile([P, count, span], F32, name="res%d_%d" % (first, m0))
+                if store_no in ON_VECTOR:
                     nc.vector.tensor_copy(res[:], acc2[:])
                 else:
                     nc.scalar.copy(res[:], acc2[:])
-                nc.sync.dma_start(out=out_view[:, m0 : m0 + count, toks], in_=res[:])
-                stores.append(res)
-                m0 += count
-
-        for first, second in ((0, 1), (2, 2), (3, 4)):
-            for i in range(first, second + 1):
-                weave(*CHUNKS[i][:2])
-            for i in range(first, second + 1):
-                quantise(*CHUNKS[i][:2])
-        for chunk in CHUNKS[:3]:
-            project(*chunk)
-        project(HALF, HALF, (1, 1, 1, 1))
+                nc.sync.dma_start(out=out_view[:, m0 : m0 + count, first : first + span], in_=res[:])
+                store_no += 1

@@ -25,17 +25,19 @@ QUADRANT = 32
 QUADRANTS = P // QUADRANT
 SCALE_ROWS = 4
 SHIFT = 16
-GATE_STEP = QUADRANT // (T // P)
 BANKS = 8
 EARLY_EXPERTS = E // 2
-MIDDLE = T // 2
 
-BYTE_CUTS = ((0, P), (P, MIDDLE), (MIDDLE, T))
-WORD_CUTS = ((0, P), (P, C), (C, 2 * C), (2 * C, 3 * C), (3 * C, T))
-SCATTER_CUTS = ((0, P), (P, C), (C, 3 * P), (3 * P, MIDDLE), (MIDDLE, 3 * C), (3 * C, T))
-QUANTISE_RUNS = (((0, P), (P, P)), ((C, C),), ((MIDDLE, C), (3 * C, C)))
-STORES = ((0, (P,), 2), (P, (P, C), 1), (MIDDLE, (MIDDLE,), 1))
-ON_VECTOR = (5, 7, 9)
+BYTE_CUTS = ((0, 128), (128, 512), (512, 1024))
+WORD_CUTS = ((0, 128), (128, 256), (256, 512), (512, 1024))
+SCATTERS = ((0, 0, 1), (1, 0, 1), (0, 1, 2), (1, 1, 3), (0, 2, 4), (1, 3, 6), (0, 4, 8), (1, 6, 8))
+CHUNKS = ((0, 128), (128, 128), (256, 256), (512, 256), (768, 256))
+FIRST_HALF_ON_GPSIMD = (512,)
+SECOND_HALF_ON_SCALAR = (256,)
+STORES = ((0, 1, 0, (128,)), (1, 3, 0, (128,))) + tuple((m, 1, 128, (128, 256)) for m in range(4)) + tuple((m, 1, 512, (256, 256)) for m in range(4))
+ON_VECTOR = (3, 5, 7, 9)
+LATE_PLACES = ("got_words0_1", "h0")
+BY_HALVES = (0,)
 
 
 def load_scale_rows(nc, plane, rows):
@@ -63,12 +65,12 @@ def tile_moe_sdn_lin_gelu_kernel(
         w2_plane = keep.tile([P, 1, N], U8, name="w2_plane", align_bytes=64)
         w2_sb = keep.tile([P, 2 * N], U8, name="w2_sb", align_bytes=64)
         c_words = keep.tile([P, T], U32, name="c_words", align_bytes=64)
+        c_scales = keep.tile([P, T], U8, name="c_scales", align_bytes=64)
         x_sb = keep.tile([P, PASSES, T], I32, name="x_sb", align_bytes=64)
         w1_sb = [keep.tile([P, PASSES, 2 * H], U8, name="w1_sb%d" % e, align_bytes=64) for e in range(EARLY_EXPERTS)]
         gate_rows = keep.tile([P, QUADRANT], F32, name="gate_rows", align_bytes=64)
         gate_cols = keep.tile([P, QUADRANT], F32, name="gate_cols", align_bytes=64)
         identity = keep.tile([P, P], F32, name="identity")
-        staged = keep.tile([P, 2, T], F32, name="staged")
         halves = [keep.tile([P, T], F32, name="plane%d" % u, align_bytes=64) for u in range(2)]
         got_scales = [keep.tile([P, hi - lo], U8, name="got_scales%d" % lo, align_bytes=64) for lo, hi in BYTE_CUTS]
         moved_scales = [keep.tile([P, hi - lo], U8, name="moved_scales%d" % lo, align_bytes=64) for lo, hi in BYTE_CUTS]
@@ -95,7 +97,6 @@ def tile_moe_sdn_lin_gelu_kernel(
             )
 
         nc.gpsimd.memset(x_plane[:].bitcast(I32), 0)
-        nc.gpsimd.memset(gate_rows[:], 0.0)
         nc.vector.memset(w1_planes[0][:].bitcast(I32), 0)
         for moved in moved_scales:
             nc.vector.memset(moved[:].bitcast(I32), 0)
@@ -104,13 +105,14 @@ def tile_moe_sdn_lin_gelu_kernel(
         make_identity(nc, identity[:])
 
         nc.sync.dma_start(offsets[:], offs)
+        nc.scalar.dma_start(
+            out=gate_rows[:],
+            in_=gate[0:QUADRANTS].rearrange("k (b a i) -> a (k b) i", a=QUADRANTS, i=QUADRANT),
+        )
         x_rows = x_scales.bitcast(I32).rearrange("s (q r) t -> r q s t", r=SCALE_ROWS)
         for r in range(SCALE_ROWS):
             queue = nc.scalar if r % 2 else nc.sync
             queue.dma_start(out=x_plane[:].bitcast(I32)[r:P:SHIFT], in_=x_rows[r])
-        nc.scalar.dma_start(
-            out=gate_rows[0:P:GATE_STEP, :], in_=gate[0].rearrange("(b a i) -> a b i", a=QUADRANTS, i=QUADRANT)
-        )
         nc.sync.dma_start(out=x_sb[:], in_=x_words.rearrange("s p t d -> p s (t d)").bitcast(I32))
         load_w1(0)
         load_w1_scales(0)
@@ -118,7 +120,8 @@ def tile_moe_sdn_lin_gelu_kernel(
         gather_scales(0)
         gather_scales(1)
         load_w1(1)
-        gather_scales(2)
+        for a in range(2, len(BYTE_CUTS)):
+            gather_scales(a)
         load_w1_scales(1)
 
         got_words = {}
@@ -129,12 +132,14 @@ def tile_moe_sdn_lin_gelu_kernel(
                 for j0 in range(lo, hi, P):
                     got_words[j0, s] = words[:, j0 - lo : j0 - lo + P]
 
+        last_words = words
+        both = keep.tile([P, 2, T], F32, name="both")
         for j0 in range(0, T, P):
             e = j0 // C
             b = j0 // P
             a = [j0 < hi for lo, hi in BYTE_CUTS].index(True)
             if e >= EARLY_EXPERTS and j0 % C == 0:
-                w1_sb.append(keep.tile([P, PASSES, 2 * H], U8, name="h%d" % (e - EARLY_EXPERTS), align_bytes=64))
+                w1_sb.append(keep.tile([P, PASSES, 2 * H], U8, name=LATE_PLACES[e - EARLY_EXPERTS], align_bytes=64))
                 load_w1(e)
             cols = slice(j0 - BYTE_CUTS[a][0], j0 - BYTE_CUTS[a][0] + P)
             acc = psum.tile([P, H], F32, name="bank%d" % b)
@@ -149,44 +154,91 @@ def tile_moe_sdn_lin_gelu_kernel(
                     stop=(s == PASSES - 1),
                 )
             h = keep.tile([P, 2, P, 2], F32, name="h%d" % b, align_bytes=64)
-            nc.scalar.activation(h[:], acc[:].rearrange("p (q u d) -> p u q d", u=2, d=2), ACT.Gelu_apprx_tanh)
-            pairs = keep.tile([P, H], BF16, name="pairs%d" % b)
-            weight = gate_cols[:, GATE_STEP * b : GATE_STEP * b + 1]
-            nc.gpsimd.tensor_scalar(pairs[:], h[:].rearrange("p u q d -> p (u q d)"), weight, 0.0, ALU.mult, ALU.add)
-            turned = psum.tile([P, 2, P], F32, name="bank%d" % b)
-            for u in range(2):
-                nc.tensor.transpose(turned[:, u, :], pairs[:].bitcast(F32)[:, u * P : (u + 1) * P], identity[:])
-            nc.scalar.copy(staged[:, :, j0 : j0 + P], turned[:])
+            pairs = keep.tile([P, 2, 2 * P], BF16, name="pairs%d" % b)
+            weight = gate_cols[:, b : b + 1]
+            sums = acc[:].rearrange("p (q u d) -> p u q d", u=2, d=2)
+            if b in BY_HALVES:
+                for u in range(2):
+                    nc.scalar.activation(h[:, u], sums[:, u], ACT.Gelu_apprx_tanh)
+                for u in range(2):
+                    nc.gpsimd.tensor_scalar(
+                        pairs[:, u, :], h[:, u].rearrange("p q d -> p (q d)"), weight, 0.0, ALU.mult, ALU.add
+                    )
+                for u in range(2):
+                    turned = psum.tile([P, P], F32, name="bank%d" % (b if u else BANKS - 1))
+                    nc.tensor.transpose(turned[:], pairs[:, u, :].bitcast(F32), identity[:])
+                    nc.scalar.copy(both[:, u, j0 : j0 + P], turned[:])
+            else:
+                nc.scalar.activation(h[:], sums, ACT.Gelu_apprx_tanh)
+                nc.gpsimd.tensor_scalar(
+                    pairs[:].rearrange("p u c -> p (u c)"),
+                    h[:].rearrange("p u q d -> p (u q d)"),
+                    weight,
+                    0.0,
+                    ALU.mult,
+                    ALU.add,
+                )
+                turned = psum.tile([P, 2, P], F32, name="bank%d" % b)
+                for u in range(2):
+                    nc.tensor.transpose(turned[:, u, :], pairs[:, u, :].bitcast(F32), identity[:])
+                nc.scalar.copy(both[:, :, j0 : j0 + P], turned[:])
 
         nc.sync.dma_start(out=w2_sb[:].bitcast(I32), in_=w2_words[0].bitcast(I32))
         load_scale_rows(nc, w2_plane, w2_scales.rearrange("s b n -> b s n"))
 
-        for lo, hi in SCATTER_CUTS:
-            for u in range(2):
-                nc.vector.tensor_copy(halves[u][:].indirect(listed(lo, hi)), staged[:, u, lo:hi])
+        for u, lo, hi in SCATTERS:
+            nc.vector.tensor_copy(halves[u][:].indirect(listed(lo * P, hi * P)), both[:, u, lo * P : hi * P])
 
         woven = {}
-        for run in QUANTISE_RUNS:
-            for t0, width in run:
-                woven[t0] = keep.tile([P, width, 2], F32, name="c_tok%d" % t0, align_bytes=64)
-                nc.scalar.copy(woven[t0][:], halves[0][:, t0 : t0 + width].unsqueeze(2).to_broadcast([P, width, 2]))
 
-        c_scales = keep.tile([P, T], U8, name="c_scales", align_bytes=64)
-        for run in QUANTISE_RUNS:
-            for t0, width in run:
-                nc.vector.tensor_copy(woven[t0][:, :, 1], halves[1][:, t0 : t0 + width])
-            for t0, width in run:
-                nc.vector.quantize_mx(
-                    out=c_words[:, t0 : t0 + width].bitcast(FP8X4),
-                    scales=c_scales[:, t0 : t0 + width],
-                    in_=woven[t0][:].rearrange("p t u -> p (t u)").bitcast(BF16),
-                )
+        def weave_first(copy, t0, width):
+            tile = keep.tile([P, 2 * width], F32, name="c_tok%d" % t0, align_bytes=64)
+            for c0 in range(0, width, P):
+                woven[t0 + c0] = tile[:, 2 * c0 : 2 * width]
+            twice = halves[0][:, t0 : t0 + width].unsqueeze(2).to_broadcast([P, width, 2])
+            copy(tile[:].rearrange("p (t u) -> p t u", u=2), twice)
+
+        def weave_second(copy, t0, width):
+            copy(woven[t0][:, 1 : 2 * width : 2], halves[1][:, t0 : t0 + width])
+
+        def quantise(t0, width):
+            nc.vector.quantize_mx(
+                out=c_words[:, t0 : t0 + width].bitcast(FP8X4),
+                scales=c_scales[:, t0 : t0 + width],
+                in_=woven[t0][:, 0 : 2 * width].bitcast(BF16),
+            )
+
+        weave_first(nc.gpsimd.tensor_copy, 0, C)
+        weave_first(nc.scalar.copy, C, C)
+        weave_first(nc.gpsimd.tensor_copy, 2 * C, C)
+        weave_second(nc.scalar.copy, C, C)
+        weave_first(nc.scalar.copy, 3 * C, C)
+        warm = psum.tile([P, H], F32, name="bank%d" % (BANKS - 1))
+        nc.tensor.transpose(warm[:, 0:P], halves[0][:, 0:P], identity[:])
+        for rep in range(4):
+            nc.tensor.matmul_mx(
+                out=warm[:],
+                lhsT=w2_sb[:, 0 : 2 * P].bitcast(FP4X4),
+                lhsT_scale=w2_plane[:, 0, 0:P],
+                rhs=last_words[:].bitcast(FP8X4),
+                rhs_scale=got_scales[-1][:],
+                start=True,
+                stop=True,
+            )
+
+        weave_second(nc.vector.tensor_copy, 0, P)
+        weave_second(nc.vector.tensor_copy, P, P)
+        quantise(0, P)
+        quantise(P, P)
+        quantise(C, C)
+        for t0 in (2 * C, 3 * C):
+            weave_second(nc.vector.tensor_copy, t0, C)
+            quantise(t0, C)
 
         out_view = out.rearrange("(m p) t -> p m t", p=P)
-        store_no = 0
-        for first, widths, count in STORES:
+        for store_no, (m0, count, first, widths) in enumerate(STORES):
             span = sum(widths)
-            for m0 in range(0, N // P, count):
+            if True:
                 acc2 = psum.tile([P, count, span], F32, name="bank%d" % (store_no % BANKS))
                 for j in range(count):
                     m = m0 + j
@@ -208,4 +260,3 @@ def tile_moe_sdn_lin_gelu_kernel(
                 else:
                     nc.scalar.copy(res[:], acc2[:])
                 nc.sync.dma_start(out=out_view[:, m0 : m0 + count, first : first + span], in_=res[:])
-                store_no += 1

@@ -213,18 +213,6 @@ def tile_moe_sdn_lin_gelu_kernel(
         weave_first(nc.gpsimd.tensor_copy, 2 * C, C)
         weave_second(nc.scalar.copy, C, C)
         weave_first(nc.scalar.copy, 3 * C, C)
-        warm = psum.tile([P, H], F32, name="bank%d" % (BANKS - 1))
-        nc.tensor.transpose(warm[:, 0:P], halves[0][:, 0:P], identity[:])
-        for rep in range(4):
-            nc.tensor.matmul_mx(
-                out=warm[:],
-                lhsT=w2_sb[:, 0 : 2 * P].bitcast(FP4X4),
-                lhsT_scale=w2_plane[:, 0, 0:P],
-                rhs=last_words[:].bitcast(FP8X4),
-                rhs_scale=got_scales[-1][:],
-                start=True,
-                stop=True,
-            )
 
         weave_second(nc.vector.tensor_copy, 0, P)
         weave_second(nc.vector.tensor_copy, P, P)

@@ -34,8 +34,8 @@ SCATTERS = ((0, 0, 1), (1, 0, 1), (0, 1, 2), (1, 1, 3), (0, 2, 4), (1, 3, 6), (0
 CHUNKS = ((0, 128), (128, 128), (256, 256), (512, 256), (768, 256))
 FIRST_HALF_ON_GPSIMD = (512,)
 SECOND_HALF_ON_SCALAR = (256,)
-STORES = ((0, 1, 0, (128,)), (1, 3, 0, (128,))) + tuple((m, 1, 128, (128, 256)) for m in range(4)) + tuple((m, 1, 512, (256, 256)) for m in range(4))
-ON_VECTOR = (3, 5, 7, 9)
+STORES = ((0, 1, 0, (128,)), (1, 1, 0, (128,)), (2, 2, 0, (128,))) + tuple((m, 1, 128, (128, 256)) for m in range(4)) + tuple((m, 1, 512, (512,)) for m in range(4))
+ON_VECTOR = (5, 7, 9)
 LATE_PLACES = ("got_words0_1", "h0")
 BY_HALVES = (0,)
 
@@ -64,7 +64,7 @@ def tile_moe_sdn_lin_gelu_kernel(
         ]
         w2_plane = keep.tile([P, 1, N], U8, name="w2_plane", align_bytes=64)
         w2_sb = keep.tile([P, 2 * N], U8, name="w2_sb", align_bytes=64)
-        c_words = keep.tile([P, T], U32, name="c_words", align_bytes=64)
+        c_words = [keep.tile([P, T // 2], U32, name="c_words", align_bytes=64)]
         c_scales = keep.tile([P, T], U8, name="c_scales", align_bytes=64)
         x_sb = keep.tile([P, PASSES, T], I32, name="x_sb", align_bytes=64)
         w1_sb = [keep.tile([P, PASSES, 2 * H], U8, name="w1_sb%d" % e, align_bytes=64) for e in range(EARLY_EXPERTS)]
@@ -203,7 +203,7 @@ def tile_moe_sdn_lin_gelu_kernel(
 
         def quantise(t0, width):
             nc.vector.quantize_mx(
-                out=c_words[:, t0 : t0 + width].bitcast(FP8X4),
+                out=c_words[t0 // 512][:, t0 % 512 : t0 % 512 + width].bitcast(FP8X4),
                 scales=c_scales[:, t0 : t0 + width],
                 in_=woven[t0][:, 0 : 2 * width].bitcast(BF16),
             )
@@ -213,7 +213,7 @@ def tile_moe_sdn_lin_gelu_kernel(
         weave_first(nc.gpsimd.tensor_copy, 2 * C, C)
         weave_second(nc.scalar.copy, C, C)
         weave_first(nc.scalar.copy, 3 * C, C)
-
+        c_words.append(keep.tile([P, T // 2], U32, name="plane0", align_bytes=64))
         weave_second(nc.vector.tensor_copy, 0, P)
         weave_second(nc.vector.tensor_copy, P, P)
         quantise(0, P)
@@ -221,6 +221,7 @@ def tile_moe_sdn_lin_gelu_kernel(
         quantise(C, C)
         for t0 in (2 * C, 3 * C):
             weave_second(nc.vector.tensor_copy, t0, C)
+        for t0 in (2 * C, 3 * C):
             quantise(t0, C)
 
         out_view = out.rearrange("(m p) t -> p m t", p=P)
@@ -236,7 +237,7 @@ def tile_moe_sdn_lin_gelu_kernel(
                             out=acc2[:, j, t0 - first : t0 - first + width],
                             lhsT=w2_sb[:, 2 * P * m : 2 * P * (m + 1)].bitcast(FP4X4),
                             lhsT_scale=w2_plane[:, 0, P * m : P * (m + 1)],
-                            rhs=c_words[:, t0 : t0 + width].bitcast(FP8X4),
+                            rhs=c_words[t0 // 512][:, t0 % 512 : t0 % 512 + width].bitcast(FP8X4),
                             rhs_scale=c_scales[:, t0 : t0 + width],
                             start=True,
                             stop=True,

@@ -30,7 +30,7 @@ EARLY_EXPERTS = E // 2
 
 BYTE_CUTS = ((0, 128), (128, 512), (512, 1024))
 WORD_CUTS = ((0, 128), (128, 256), (256, 512), (512, 1024))
-SCATTERS = ((0, 0, 1), (1, 0, 1), (0, 1, 2), (1, 1, 3), (0, 2, 4), (1, 3, 6), (0, 4, 8), (1, 6, 8))
+SCATTERS = ((0, 0, 1), (1, 0, 1), (0, 1, 2), (1, 1, 2), (0, 2, 3), (1, 2, 4), (0, 3, 5), (1, 4, 6), (0, 5, 8), (1, 6, 8))
 CHUNKS = ((0, 128), (128, 128), (256, 256), (512, 256), (768, 256))
 FIRST_HALF_ON_GPSIMD = (512,)
 SECOND_HALF_ON_SCALAR = (256,)

@@ -40,9 +40,9 @@ LATE_PLACES = ("got_words0_1", "h0")
 BY_HALVES = (0,)
 
 
-def load_scale_rows(nc, plane, rows):
+def load_scale_rows(queue, plane, rows):
     for r in range(SCALE_ROWS):
-        nc.sync.dma_start(
+        queue.dma_start(
             out=plane[:].bitcast(I32)[r:P:QUADRANT],
             in_=rows.bitcast(I32)[r : QUADRANTS * SCALE_ROWS : SCALE_ROWS],
         )
@@ -82,7 +82,7 @@ def tile_moe_sdn_lin_gelu_kernel(
 
         def load_w1_scales(g):
             experts = w1_scales[g * EARLY_EXPERTS : (g + 1) * EARLY_EXPERTS]
-            load_scale_rows(nc, w1_planes[g], experts.rearrange("e s b i -> b (e s) i"))
+            load_scale_rows(nc.sync if g else nc.scalar, w1_planes[g], experts.rearrange("e s b i -> b (e s) i"))
 
         def listed(lo, hi):
             return offsets[:, lo // LIST_ROWS : hi // LIST_ROWS]
@@ -184,7 +184,7 @@ def tile_moe_sdn_lin_gelu_kernel(
                 nc.scalar.copy(both[:, :, j0 : j0 + P], turned[:])
 
         nc.sync.dma_start(out=w2_sb[:].bitcast(I32), in_=w2_words[0].bitcast(I32))
-        load_scale_rows(nc, w2_plane, w2_scales.rearrange("s b n -> b s n"))
+        load_scale_rows(nc.sync, w2_plane, w2_scales.rearrange("s b n -> b s n"))
 
         for u, lo, hi in SCATTERS:
             nc.vector.tensor_copy(halves[u][:].indirect(listed(lo * P, hi * P)), both[:, u, lo * P : hi * P])
@@ -210,7 +210,7 @@ def tile_moe_sdn_lin_gelu_kernel(
 
         weave_first(nc.gpsimd.tensor_copy, 0, C)
         weave_first(nc.scalar.copy, C, C)
-        weave_first(nc.gpsimd.tensor_copy, 2 * C, C)
+        weave_first(nc.scalar.copy, 2 * C, C)
         weave_second(nc.scalar.copy, C, C)
         weave_first(nc.scalar.copy, 3 * C, C)
         c_words.append(keep.tile([P, T // 2], U32, name="plane0", align_bytes=64))

@@ -30,12 +30,12 @@ EARLY_EXPERTS = E // 2
 
 BYTE_CUTS = ((0, 128), (128, 512), (512, 1024))
 WORD_CUTS = ((0, 128), (128, 256), (256, 512), (512, 1024))
-SCATTERS = ((0, 0, 1), (1, 0, 1), (0, 1, 2), (1, 1, 2), (0, 2, 3), (1, 2, 4), (0, 3, 5), (1, 4, 6), (0, 5, 8), (1, 6, 8))
+SCATTERS = ((0, 0, 128), (1, 0, 128), (0, 128, 256), (1, 128, 256), (0, 256, 384), (1, 256, 512), (0, 384, 640), (1, 512, 672), (0, 640, 1024), (1, 672, 1024))
 CHUNKS = ((0, 128), (128, 128), (256, 256), (512, 256), (768, 256))
 FIRST_HALF_ON_GPSIMD = (512,)
 SECOND_HALF_ON_SCALAR = (256,)
-STORES = ((0, 1, 0, (128,)), (1, 1, 0, (128,)), (2, 2, 0, (128,))) + tuple((m, 1, 128, (128, 256)) for m in range(4)) + tuple((m, 1, 512, (512,)) for m in range(4))
-ON_VECTOR = (5, 7, 9)
+STORES = ((0, 1, 0, (128,)), (1, 1, 0, (128,)), (2, 1, 0, (256,)), (3, 1, 0, (256,)), (0, 1, 128, (128, 256)), (1, 1, 128, (128, 256)), (2, 2, 256, (256,))) + tuple((m, 1, 512, (512,)) for m in range(4))
+ON_VECTOR = (7, 9)
 LATE_PLACES = ("got_words0_1", "h0")
 BY_HALVES = (0,)
 
@@ -187,7 +187,7 @@ def tile_moe_sdn_lin_gelu_kernel(
         load_scale_rows(nc.sync, w2_plane, w2_scales.rearrange("s b n -> b s n"))
 
         for u, lo, hi in SCATTERS:
-            nc.vector.tensor_copy(halves[u][:].indirect(listed(lo * P, hi * P)), both[:, u, lo * P : hi * P])
+            nc.vector.tensor_copy(halves[u][:].indirect(listed(lo, hi)), both[:, u, lo:hi])
 
         woven = {}
 
@@ -208,11 +208,25 @@ def tile_moe_sdn_lin_gelu_kernel(
                 in_=woven[t0][:, 0 : 2 * width].bitcast(BF16),
             )
 
-        weave_first(nc.gpsimd.tensor_copy, 0, C)
+        weave_first(nc.scalar.copy, 0, C)
         weave_first(nc.scalar.copy, C, C)
-        weave_first(nc.scalar.copy, 2 * C, C)
+        late = keep.tile([P, T], F32, name="c_tok512", align_bytes=64)
+        for t0 in (2 * C, 3 * C):
+            woven[t0] = late[:, 2 * (t0 - 2 * C) : T]
+        nc.scalar.copy(
+            late[:, 0 : 2 * P].rearrange("p (t u) -> p t u", u=2),
+            halves[0][:, 2 * C : 2 * C + P].unsqueeze(2).to_broadcast([P, P, 2]),
+        )
+        rest = halves[0][:, 2 * C + P : T].bitcast(BF16).rearrange("p (t d) -> p t d", d=2)
+        nc.gpsimd.tensor_scalar(
+            late[:, 2 * P : T].bitcast(BF16).rearrange("p (t u d) -> p t u d", u=2, d=2),
+            rest.unsqueeze(2).to_broadcast([P, T - 2 * C - P, 2, 2]),
+            1.0,
+            0.0,
+            ALU.mult,
+            ALU.add,
+        )
         weave_second(nc.scalar.copy, C, C)
-        weave_first(nc.scalar.copy, 3 * C, C)
         c_words.append(keep.tile([P, T // 2], U32, name="plane0", align_bytes=64))
         weave_second(nc.vector.tensor_copy, 0, P)
         weave_second(nc.vector.tensor_copy, P, P)

@@ -29,7 +29,7 @@ BANKS = 8
 EARLY_EXPERTS = E // 2
 
 BYTE_CUTS = ((0, 128), (128, 512), (512, 1024))
-WORD_CUTS = ((0, 128), (128, 256), (256, 512), (512, 1024))
+WORD_CUTS = ((0, 128), (128, 256), (256, 512), (512, 768), (768, 1024))
 SCATTERS = ((0, 0, 128), (1, 0, 128), (0, 128, 256), (1, 128, 256), (0, 256, 384), (1, 256, 512), (0, 384, 640), (1, 512, 672), (0, 640, 1024), (1, 672, 1024))
 CHUNKS = ((0, 128), (128, 128), (256, 256), (512, 256), (768, 256))
 FIRST_HALF_ON_GPSIMD = (512,)

@@ -38,6 +38,7 @@ STORES = ((0, 1, 0, (128,)), (1, 1, 0, (128,)), (2, 1, 0, (256,)), (3, 1, 0, (25
 ON_VECTOR = (7, 9)
 LATE_PLACES = ("got_words0_1", "h0")
 BY_HALVES = (0,)
+SEAM = (752, 784)
 
 
 def load_scale_rows(queue, plane, rows):
@@ -189,14 +190,13 @@ def tile_moe_sdn_lin_gelu_kernel(
         for u, lo, hi in SCATTERS:
             nc.vector.tensor_copy(halves[u][:].indirect(listed(lo, hi)), both[:, u, lo:hi])
 
-        woven = {}
+        start = keep.tile([P, 2 * C], F32, name="c_tok0", align_bytes=64)
+        rest = keep.tile([P, 2 * (T - C)], F32, name="c_tok256", align_bytes=64)
+        woven = {0: start[:], P: start[:, 2 * P :], C: rest[:], 2 * C: rest[:, 2 * C :], 3 * C: rest[:, 4 * C :]}
 
-        def weave_first(copy, t0, width):
-            tile = keep.tile([P, 2 * width], F32, name="c_tok%d" % t0, align_bytes=64)
-            for c0 in range(0, width, P):
-                woven[t0 + c0] = tile[:, 2 * c0 : 2 * width]
+        def weave_first(t0, width, place):
             twice = halves[0][:, t0 : t0 + width].unsqueeze(2).to_broadcast([P, width, 2])
-            copy(tile[:].rearrange("p (t u) -> p t u", u=2), twice)
+            nc.scalar.copy(place[:, 0 : 2 * width].rearrange("p (t u) -> p t u", u=2), twice)
 
         def weave_second(copy, t0, width):
             copy(woven[t0][:, 1 : 2 * width : 2], halves[1][:, t0 : t0 + width])
@@ -208,25 +208,11 @@ def tile_moe_sdn_lin_gelu_kernel(
                 in_=woven[t0][:, 0 : 2 * width].bitcast(BF16),
             )
 
-        weave_first(nc.scalar.copy, 0, C)
-        weave_first(nc.scalar.copy, C, C)
-        late = keep.tile([P, T], F32, name="c_tok512", align_bytes=64)
-        for t0 in (2 * C, 3 * C):
-            woven[t0] = late[:, 2 * (t0 - 2 * C) : T]
-        nc.scalar.copy(
-            late[:, 0 : 2 * P].rearrange("p (t u) -> p t u", u=2),
-            halves[0][:, 2 * C : 2 * C + P].unsqueeze(2).to_broadcast([P, P, 2]),
-        )
-        rest = halves[0][:, 2 * C + P : T].bitcast(BF16).rearrange("p (t d) -> p t d", d=2)
-        nc.gpsimd.tensor_scalar(
-            late[:, 2 * P : T].bitcast(BF16).rearrange("p (t u d) -> p t u d", u=2, d=2),
-            rest.unsqueeze(2).to_broadcast([P, T - 2 * C - P, 2, 2]),
-            1.0,
-            0.0,
-            ALU.mult,
-            ALU.add,
-        )
+        weave_first(0, C, woven[0])
+        weave_first(C, SEAM[0] - C, woven[C])
+        weave_first(SEAM[1], T - SEAM[1], rest[:, 2 * (SEAM[1] - C) :])
         weave_second(nc.scalar.copy, C, C)
+        weave_first(SEAM[0], SEAM[1] - SEAM[0], rest[:, 2 * (SEAM[0] - C) :])
         c_words.append(keep.tile([P, T // 2], U32, name="plane0", align_bytes=64))
         weave_second(nc.vector.tensor_copy, 0, P)
         weave_second(nc.vector.tensor_copy, P, P)

@@ -29,13 +29,13 @@ BANKS = 8
 EARLY_EXPERTS = E // 2
 
 BYTE_CUTS = ((0, 128), (128, 512), (512, 1024))
-WORD_CUTS = ((0, 128), (128, 256), (256, 512), (512, 768), (768, 1024))
-SCATTERS = ((0, 0, 128), (1, 0, 128), (0, 128, 256), (1, 128, 256), (0, 256, 384), (1, 256, 512), (0, 384, 640), (1, 512, 672), (0, 640, 1024), (1, 672, 1024))
+WORD_CUTS = ((0, 128), (128, 256), (256, 512), (512, 1024))
+SCATTERS = ((0, 0, 128), (1, 0, 128), (0, 128, 256), (1, 128, 256), (0, 256, 384), (1, 256, 448), (0, 384, 640), (1, 448, 640), (0, 640, 1024), (1, 640, 1024))
 CHUNKS = ((0, 128), (128, 128), (256, 256), (512, 256), (768, 256))
 FIRST_HALF_ON_GPSIMD = (512,)
 SECOND_HALF_ON_SCALAR = (256,)
 STORES = ((0, 1, 0, (128,)), (1, 1, 0, (128,)), (2, 1, 0, (256,)), (3, 1, 0, (256,)), (0, 1, 128, (128, 256)), (1, 1, 128, (128, 256)), (2, 2, 256, (256,))) + tuple((m, 1, 512, (512,)) for m in range(4))
-ON_VECTOR = (7, 9)
+ON_VECTOR = (5, 7, 9)
 LATE_PLACES = ("got_words0_1", "h0")
 BY_HALVES = (0,)
 SEAM = (752, 784)
@@ -192,7 +192,7 @@ def tile_moe_sdn_lin_gelu_kernel(
 
         start = keep.tile([P, 2 * C], F32, name="c_tok0", align_bytes=64)
         rest = keep.tile([P, 2 * (T - C)], F32, name="c_tok256", align_bytes=64)
-        woven = {0: start[:], P: start[:, 2 * P :], C: rest[:], 2 * C: rest[:, 2 * C :], 3 * C: rest[:, 4 * C :]}
+        woven = {0: start[:], P: start[:, 2 * P :], C: rest[:], 2 * C: rest[:, 2 * C :], 2 * C + P: rest[:, 2 * C + 2 * P :], 3 * C: rest[:, 4 * C :]}
 
         def weave_first(t0, width, place):
             twice = halves[0][:, t0 : t0 + width].unsqueeze(2).to_broadcast([P, width, 2])
@@ -213,14 +213,15 @@ def tile_moe_sdn_lin_gelu_kernel(
         weave_first(SEAM[1], T - SEAM[1], rest[:, 2 * (SEAM[1] - C) :])
         weave_second(nc.scalar.copy, C, C)
         weave_first(SEAM[0], SEAM[1] - SEAM[0], rest[:, 2 * (SEAM[0] - C) :])
+        weave_second(nc.scalar.copy, 2 * C, P)
         c_words.append(keep.tile([P, T // 2], U32, name="plane0", align_bytes=64))
         weave_second(nc.vector.tensor_copy, 0, P)
         weave_second(nc.vector.tensor_copy, P, P)
         quantise(0, P)
         quantise(P, P)
         quantise(C, C)
-        for t0 in (2 * C, 3 * C):
-            weave_second(nc.vector.tensor_copy, t0, C)
+        weave_second(nc.vector.tensor_copy, 2 * C + P, P)
+        weave_second(nc.vector.tensor_copy, 3 * C, C)
         for t0 in (2 * C, 3 * C):
             quantise(t0, C)
 

@@ -29,7 +29,7 @@ BANKS = 8
 EARLY_EXPERTS = E // 2
 
 BYTE_CUTS = ((0, 128), (128, 512), (512, 1024))
-WORD_CUTS = ((0, 128), (128, 256), (256, 512), (512, 1024))
+WORD_CUTS = ((0, 128), (128, 256), (256, 512), (512, 768), (768, 1024))
 SCATTERS = ((0, 0, 128), (1, 0, 128), (0, 128, 256), (1, 128, 256), (0, 256, 384), (1, 256, 448), (0, 384, 640), (1, 448, 640), (0, 640, 1024), (1, 640, 1024))
 CHUNKS = ((0, 128), (128, 128), (256, 256), (512, 256), (768, 256))
 FIRST_HALF_ON_GPSIMD = (512,)

@@ -26,6 +26,7 @@ QUADRANTS = P // QUADRANT
 SCALE_ROWS = 4
 SHIFT = 16
 BANKS = 8
+LONGEST = 256
 EARLY_EXPERTS = E // 2
 
 BYTE_CUTS = ((0, 128), (128, 512), (512, 1024))
@@ -90,7 +91,9 @@ def tile_moe_sdn_lin_gelu_kernel(
 
         def gather_scales(a):
             lo, hi = BYTE_CUTS[a]
-            nc.vector.tensor_copy(got_scales[a][:], x_plane[:].indirect(listed(lo, hi)))
+            for j0 in range(lo, hi, LONGEST):
+                j1 = min(j0 + LONGEST, hi)
+                nc.vector.tensor_copy(got_scales[a][:, j0 - lo : j1 - lo], x_plane[:].indirect(listed(j0, j1)))
             queue = nc.scalar if a == 0 else nc.sync
             queue.dma_start(
                 out=moved_scales[a][:].bitcast(I32)[0 : P - SHIFT],

from contextlib import ExitStack

import concourse.mybir as mybir
from concourse.masks import make_identity

K, T, E, C, H, N = 1024, 1024, 4, 256, 512, 512
FLOPS = 2 * K * H * E * C + 2 * H * N * T

F32 = mybir.dt.float32
BF16 = mybir.dt.bfloat16
I32 = mybir.dt.int32
U32 = mybir.dt.uint32
U16 = mybir.dt.uint16
U8 = mybir.dt.uint8
FP8X4 = mybir.dt.float8_e4m3fn_x4
FP4X4 = mybir.dt.float4_e2m1fn_x4
ACT = mybir.ActivationFunctionType
ALU = mybir.AluOpType

P = 128
PACK = 4
PASSES = K // (P * PACK)
LIST_ROWS = 16
QUADRANT = 32
QUADRANTS = P // QUADRANT
SCALE_ROWS = 4
SHIFT = 16
BANKS = 8
LONGEST = 256
EARLY_EXPERTS = E // 2

BYTE_CUTS = ((0, 128), (128, 512), (512, 1024))
WORD_CUTS = ((0, 128), (128, 256), (256, 512), (512, 768), (768, 1024))
SCATTERS = ((0, 0, 128), (1, 0, 128), (0, 128, 256), (1, 128, 256), (0, 256, 384), (1, 256, 448), (0, 384, 640), (1, 448, 640), (0, 640, 1024), (1, 640, 1024))
CHUNKS = ((0, 128), (128, 128), (256, 256), (512, 256), (768, 256))
FIRST_HALF_ON_GPSIMD = (512,)
SECOND_HALF_ON_SCALAR = (256,)
STORES = ((0, 1, 0, (128,)), (1, 1, 0, (128,)), (2, 1, 0, (256,)), (3, 1, 0, (256,)), (0, 1, 128, (128, 256)), (1, 1, 128, (128, 256)), (2, 2, 256, (256,))) + tuple((m, 1, 512, (512,)) for m in range(4))
ON_VECTOR = (5, 7, 9)
LATE_PLACES = ("got_words0_1", "h0")
BY_HALVES = (0,)
SEAM = (752, 784)


def load_scale_rows(queue, plane, rows):
    for r in range(SCALE_ROWS):
        queue.dma_start(
            out=plane[:].bitcast(I32)[r:P:QUADRANT],
            in_=rows.bitcast(I32)[r : QUADRANTS * SCALE_ROWS : SCALE_ROWS],
        )


def tile_moe_sdn_lin_gelu_kernel(
    tc, x_words, x_scales, w1_words, w1_scales, w2_words, w2_scales, gate, offs, out
):
    nc = tc.nc
    with ExitStack() as ctx:
        keep = ctx.enter_context(tc.tile_pool(name="keep", bufs=1))
        psum = ctx.enter_context(tc.psum_pool(name="psum", bufs=1))

        offsets = keep.tile([P, T // LIST_ROWS], U16, name="offsets")
        x_plane = keep.tile([P, T], U8, name="x_plane", align_bytes=64)
        w1_planes = [
            keep.tile([P, EARLY_EXPERTS * PASSES, H], U8, name="w1_plane%d" % g, align_bytes=64)
            for g in range(E // EARLY_EXPERTS)
        ]
        w2_plane = keep.tile([P, 1, N], U8, name="w2_plane", align_bytes=64)
        w2_sb = keep.tile([P, 2 * N], U8, name="w2_sb", align_bytes=64)
        c_words = [keep.tile([P, T // 2], U32, name="c_words", align_bytes=64)]
        c_scales = keep.tile([P, T], U8, name="c_scales", align_bytes=64)
        x_sb = keep.tile([P, PASSES, T], I32, name="x_sb", align_bytes=64)
        w1_sb = [keep.tile([P, PASSES, 2 * H], U8, name="w1_sb%d" % e, align_bytes=64) for e in range(EARLY_EXPERTS)]
        gate_rows = keep.tile([P, QUADRANT], F32, name="gate_rows", align_bytes=64)
        gate_cols = keep.tile([P, QUADRANT], F32, name="gate_cols", align_bytes=64)
        identity = keep.tile([P, P], F32, name="identity")
        halves = [keep.tile([P, T], F32, name="plane%d" % u, align_bytes=64) for u in range(2)]
        got_scales = [keep.tile([P, hi - lo], U8, name="got_scales%d" % lo, align_bytes=64) for lo, hi in BYTE_CUTS]
        moved_scales = [keep.tile([P, hi - lo], U8, name="moved_scales%d" % lo, align_bytes=64) for lo, hi in BYTE_CUTS]

        def load_w1(e):
            nc.sync.dma_start(
                out=w1_sb[e][:].bitcast(I32), in_=w1_words[e].rearrange("s p b -> p s b").bitcast(I32)
            )

        def load_w1_scales(g):
            experts = w1_scales[g * EARLY_EXPERTS : (g + 1) * EARLY_EXPERTS]
            load_scale_rows(nc.sync if g else nc.scalar, w1_planes[g], experts.rearrange("e s b i -> b (e s) i"))

        def listed(lo, hi):
            return offsets[:, lo // LIST_ROWS : hi // LIST_ROWS]

        def gather_scales(a):
            lo, hi = BYTE_CUTS[a]
            for j0 in range(lo, hi, LONGEST):
                j1 = min(j0 + LONGEST, hi)
                nc.vector.tensor_copy(got_scales[a][:, j0 - lo : j1 - lo], x_plane[:].indirect(listed(j0, j1)))
            queue = nc.scalar if a == 0 else nc.sync
            queue.dma_start(
                out=moved_scales[a][:].bitcast(I32)[0 : P - SHIFT],
                in_=got_scales[a][:].bitcast(I32)[SHIFT:P],
            )

        nc.gpsimd.memset(x_plane[:].bitcast(I32), 0)
        nc.vector.memset(w1_planes[0][:].bitcast(I32), 0)
        for moved in moved_scales:
            nc.vector.memset(moved[:].bitcast(I32), 0)
        nc.vector.memset(w1_planes[1][:].bitcast(I32), 0)
        nc.vector.memset(w2_plane[:].bitcast(I32), 0)
        make_identity(nc, identity[:])

        nc.sync.dma_start(offsets[:], offs)
        nc.scalar.dma_start(
            out=gate_rows[:],
            in_=gate[0:QUADRANTS].rearrange("k (b a i) -> a (k b) i", a=QUADRANTS, i=QUADRANT),
        )
        x_rows = x_scales.bitcast(I32).rearrange("s (q r) t -> r q s t", r=SCALE_ROWS)
        for r in range(SCALE_ROWS):
            queue = nc.scalar if r % 2 else nc.sync
            queue.dma_start(out=x_plane[:].bitcast(I32)[r:P:SHIFT], in_=x_rows[r])
        nc.sync.dma_start(out=x_sb[:], in_=x_words.rearrange("s p t d -> p s (t d)").bitcast(I32))
        load_w1(0)
        load_w1_scales(0)
        nc.vector.transpose(gate_cols[:], gate_rows[:])
        gather_scales(0)
        gather_scales(1)
        load_w1(1)
        for a in range(2, len(BYTE_CUTS)):
            gather_scales(a)
        load_w1_scales(1)

        got_words = {}
        for lo, hi in WORD_CUTS:
            for s in range(PASSES):
                words = keep.tile([P, hi - lo], U32, name="got_words%d_%d" % (lo, s), align_bytes=64)
                nc.vector.tensor_copy(words[:], x_sb[:, s, :].bitcast(U32).indirect(listed(lo, hi)))
                for j0 in range(lo, hi, P):
                    got_words[j0, s] = words[:, j0 - lo : j0 - lo + P]

        last_words = words
        both = keep.tile([P, 2, T], F32, name="both")
        for j0 in range(0, T, P):
            e = j0 // C
            b = j0 // P
            a = [j0 < hi for lo, hi in BYTE_CUTS].index(True)
            if e >= EARLY_EXPERTS and j0 % C == 0:
                w1_sb.append(keep.tile([P, PASSES, 2 * H], U8, name=LATE_PLACES[e - EARLY_EXPERTS], align_bytes=64))
                load_w1(e)
            cols = slice(j0 - BYTE_CUTS[a][0], j0 - BYTE_CUTS[a][0] + P)
            acc = psum.tile([P, H], F32, name="bank%d" % b)
            for s, scales in enumerate((got_scales, moved_scales)):
                nc.tensor.matmul_mx(
                    out=acc[:],
                    lhsT=got_words[j0, s].bitcast(FP8X4),
                    lhsT_scale=scales[a][:, cols],
                    rhs=w1_sb[e][:, s, :].bitcast(FP4X4),
                    rhs_scale=w1_planes[e // EARLY_EXPERTS][:, e % EARLY_EXPERTS * PASSES + s, :],
                    start=(s == 0),
                    stop=(s == PASSES - 1),
                )
            h = keep.tile([P, 2, P, 2], F32, name="h%d" % b, align_bytes=64)
            pairs = keep.tile([P, 2, 2 * P], BF16, name="pairs%d" % b)
            weight = gate_cols[:, b : b + 1]
            sums = acc[:].rearrange("p (q u d) -> p u q d", u=2, d=2)
            if b in BY_HALVES:
                for u in range(2):
                    nc.scalar.activation(h[:, u], sums[:, u], ACT.Gelu_apprx_tanh)
                for u in range(2):
                    nc.gpsimd.tensor_scalar(
                        pairs[:, u, :], h[:, u].rearrange("p q d -> p (q d)"), weight, 0.0, ALU.mult, ALU.add
                    )
                for u in range(2):
                    turned = psum.tile([P, P], F32, name="bank%d" % (b if u else BANKS - 1))
                    nc.tensor.transpose(turned[:], pairs[:, u, :].bitcast(F32), identity[:])
                    nc.scalar.copy(both[:, u, j0 : j0 + P], turned[:])
            else:
                nc.scalar.activation(h[:], sums, ACT.Gelu_apprx_tanh)
                nc.gpsimd.tensor_scalar(
                    pairs[:].rearrange("p u c -> p (u c)"),
                    h[:].rearrange("p u q d -> p (u q d)"),
                    weight,
                    0.0,
                    ALU.mult,
                    ALU.add,
                )
                turned = psum.tile([P, 2, P], F32, name="bank%d" % b)
                for u in range(2):
                    nc.tensor.transpose(turned[:, u, :], pairs[:, u, :].bitcast(F32), identity[:])
                nc.scalar.copy(both[:, :, j0 : j0 + P], turned[:])

        nc.sync.dma_start(out=w2_sb[:].bitcast(I32), in_=w2_words[0].bitcast(I32))
        load_scale_rows(nc.sync, w2_plane, w2_scales.rearrange("s b n -> b s n"))

        for u, lo, hi in SCATTERS:
            nc.vector.tensor_copy(halves[u][:].indirect(listed(lo, hi)), both[:, u, lo:hi])

        start = keep.tile([P, 2 * C], F32, name="c_tok0", align_bytes=64)
        rest = keep.tile([P, 2 * (T - C)], F32, name="c_tok256", align_bytes=64)
        woven = {0: start[:], P: start[:, 2 * P :], C: rest[:], 2 * C: rest[:, 2 * C :], 2 * C + P: rest[:, 2 * C + 2 * P :], 3 * C: rest[:, 4 * C :]}

        def weave_first(t0, width, place):
            twice = halves[0][:, t0 : t0 + width].unsqueeze(2).to_broadcast([P, width, 2])
            nc.scalar.copy(place[:, 0 : 2 * width].rearrange("p (t u) -> p t u", u=2), twice)

        def weave_second(copy, t0, width):
            copy(woven[t0][:, 1 : 2 * width : 2], halves[1][:, t0 : t0 + width])

        def quantise(t0, width):
            nc.vector.quantize_mx(
                out=c_words[t0 // 512][:, t0 % 512 : t0 % 512 + width].bitcast(FP8X4),
                scales=c_scales[:, t0 : t0 + width],
                in_=woven[t0][:, 0 : 2 * width].bitcast(BF16),
            )

        weave_first(0, C, woven[0])
        weave_first(C, SEAM[0] - C, woven[C])
        weave_first(SEAM[1], T - SEAM[1], rest[:, 2 * (SEAM[1] - C) :])
        weave_second(nc.scalar.copy, C, C)
        weave_first(SEAM[0], SEAM[1] - SEAM[0], rest[:, 2 * (SEAM[0] - C) :])
        weave_second(nc.scalar.copy, 2 * C, P)
        c_words.append(keep.tile([P, T // 2], U32, name="plane0", align_bytes=64))
        weave_second(nc.vector.tensor_copy, 0, P)
        weave_second(nc.vector.tensor_copy, P, P)
        quantise(0, P)
        quantise(P, P)
        quantise(C, C)
        weave_second(nc.vector.tensor_copy, 2 * C + P, P)
        weave_second(nc.vector.tensor_copy, 3 * C, C)
        for t0 in (2 * C, 3 * C):
            quantise(t0, C)

        out_view = out.rearrange("(m p) t -> p m t", p=P)
        for store_no, (m0, count, first, widths) in enumerate(STORES):
            span = sum(widths)
            if True:
                acc2 = psum.tile([P, count, span], F32, name="bank%d" % (store_no % BANKS))
                for j in range(count):
                    m = m0 + j
                    t0 = first
                    for width in widths:
                        nc.tensor.matmul_mx(
                            out=acc2[:, j, t0 - first : t0 - first + width],
                            lhsT=w2_sb[:, 2 * P * m : 2 * P * (m + 1)].bitcast(FP4X4),
                            lhsT_scale=w2_plane[:, 0, P * m : P * (m + 1)],
                            rhs=c_words[t0 // 512][:, t0 % 512 : t0 % 512 + width].bitcast(FP8X4),
                            rhs_scale=c_scales[:, t0 : t0 + width],
                            start=True,
                            stop=True,
                        )
                        t0 += width
                res = keep.tile([P, count, span], F32, name="res%d_%d" % (first, m0))
                if store_no in ON_VECTOR:
                    nc.vector.tensor_copy(res[:], acc2[:])
                else:
                    nc.scalar.copy(res[:], acc2[:])
                nc.sync.dma_start(out=out_view[:, m0 : m0 + count, first : first + span], in_=res[:])
